import numpy as np
import ml_dtypes


def mxq(x, axis, fmt="e4m3"):
    dtype, down = {"e4m3": (ml_dtypes.float8_e4m3fn, 7), "e5m2": (ml_dtypes.float8_e5m2, 14)}[fmt]
    v = np.moveaxis(np.asarray(x, np.float32).astype(ml_dtypes.bfloat16).astype(np.float64), axis, -1)
    blocks = v.reshape(v.shape[:-1] + (-1, 32))
    amax = np.abs(blocks).max(-1, keepdims=True)
    byte = np.maximum(np.where(amax > 0, np.frexp(amax)[1] - 1 + 127, 0) - down, 1)
    scale = np.exp2(byte - 127.0)
    codes = (blocks / scale).astype(np.float32).astype(dtype).astype(np.float64)
    return np.moveaxis((codes * scale).reshape(v.shape), -1, axis)


WIDE = False


def mx_kscale(k):
    if not WIDE:
        return np.ones(k)
    levels = np.array([10, -10, 5, -5, 0])
    if k % 512:
        return np.exp2(np.random.permutation(np.resize(levels, k // 32))).repeat(32)
    a = np.empty((k // 512, 16))
    for p in range(k // 512):
        a[p, :8] = np.random.permutation(np.resize(levels, 8))
        for g in range(8):
            far = levels[np.abs(levels - a[p, g]) >= 10]
            a[p, g + 8] = far[np.random.randint(len(far))]
    return np.exp2(a.ravel()).repeat(32)


def f64(x):
    return np.asarray(x).astype(np.float64)


def striped(idx):
    return np.tile(idx.reshape(-1, 16).T, (8, 1)).astype(np.uint16)


def unstriped(offs):
    return offs[:16].T.reshape(-1).astype(np.int64)


K, T, E, C, N = 512, 2048, 8, 256, 128


def by_expert(wq, xq):
    return np.concatenate([wq[e].T @ xq[:, e * C:(e + 1) * C] for e in range(E)], axis=1)


def setup_inputs():
    n = np.random.standard_normal
    s = mx_kscale(K)[:, None]
    return {
        "xT": (n((K, T)) * s).astype(np.float32),
        "w": (n((E, K, N)) / np.sqrt(K) / s[None]).astype(np.float32),
        "gate": np.tile(np.random.uniform(0.2, 1.0, E * C), (N, 1)).astype(np.float32),
        "offs": striped(np.random.permutation(T)[:E * C]),
    }


def reference(xT, w, gate, offs):
    idx = unstriped(offs)
    xq = mxq(f64(xT)[:, idx], 0, "e4m3")
    y = by_expert(mxq(f64(w), 1, "e4m3"), xq)
    out = np.zeros((N, T))
    out[:, idx] = f64(gate) * y
    return out

@@ -1,0 +1,163 @@
+from contextlib import ExitStack
+
+import concourse.mybir as mybir
+
+K, T, E, C, N = 512, 2048, 8, 256, 128
+FLOPS = 2 * K * N * E * C
+
+F32 = mybir.dt.float32
+BF16 = mybir.dt.bfloat16
+U32 = mybir.dt.uint32
+U16 = mybir.dt.uint16
+U8 = mybir.dt.uint8
+FP8X4 = mybir.dt.float8_e4m3fn_x4
+MULT = mybir.AluOpType.mult
+COPY = mybir.ActivationFunctionType.Copy
+
+P = 128
+CH = 512
+NCH = T // CH
+PIECE = 512
+NP = E * C // PIECE
+EPP = PIECE // C
+
+
+def tile_routed_moe_kernel(tc, xT, w, gate, offs, out):
+    nc = tc.nc
+    with ExitStack() as ctx:
+        keep = ctx.enter_context(tc.tile_pool(name="keep", bufs=1))
+        psum = ctx.enter_context(tc.psum_pool(name="psum", bufs=1))
+
+        offsets = keep.tile([P, E * C // 16], U16, name="offsets")
+        nc.sync.dma_start(offsets[:], offs)
+
+        xv = xT.rearrange("(p t) n -> p t n", t=4)
+        raw_v = keep.tile([P, 2, T], F32, name="raw_v")
+        raw_s = [keep.tile([P, 2, CH], F32, name="raw_s%d" % c) for c in range(NCH)]
+        wv = w.rearrange("e (p j) n -> p e (j n)", j=4)
+        wraw = [keep.tile([P, EPP, 4 * N], F32, name="wraw%d" % q) for q in range(NP)]
+        gate_sb = keep.tile([P, E * C], F32, name="gate_sb")
+
+        def load_v(t):
+            nc.sync.dma_start(raw_v[:, t, :], xv[:, t, :])
+
+        def load_s():
+            for c in range(NCH):
+                nc.sync.dma_start(raw_s[c][:], xv[:, 2:4, c * CH : (c + 1) * CH])
+
+        def load_w(q):
+            nc.sync.dma_start(wraw[q][:], wv[:, q * EPP : (q + 1) * EPP, :])
+
+        load_v(0)
+        load_v(1)
+        load_s()
+        load_w(0)
+        load_w(1)
+        load_w(2)
+        load_w(3)
+        nc.sync.dma_start(gate_sb[:], gate)
+
+        xb = keep.tile([P, 2, T], BF16, name="xb")
+        grouped = [keep.tile([P, 4 * PIECE], BF16, name="grouped%d" % q, align_bytes=64) for q in range(NP)]
+        wgrouped = [keep.tile([P, EPP * 4 * N], BF16, name="wgrouped%d" % q, align_bytes=64) for q in range(NP)]
+        wcodes = [keep.tile([P, EPP * N], U32, name="wcodes%d" % q, align_bytes=64) for q in range(NP)]
+        wscales = [keep.tile([P, EPP * N], U8, name="wscales%d" % q, align_bytes=64) for q in range(NP)]
+        xcodes = [keep.tile([P, PIECE], U32, name="xcodes%d" % q, align_bytes=64) for q in range(NP)]
+        xscales = [keep.tile([P, PIECE], U8, name="xscales%d" % q, align_bytes=64) for q in range(NP)]
+        acc = [psum.tile([P, PIECE], F32, name="acc%d" % q) for q in range(NP)]
+        sums = [keep.tile([P, PIECE], F32, name="sums%d" % q) for q in range(NP)]
+        window = keep.tile([P, T], F32, name="window")
+
+        def cast():
+            for c in range(NCH):
+                nc.scalar.copy(out=xb[:, :, c * CH : (c + 1) * CH], in_=raw_s[c][:])
+
+        def cols(q):
+            return offsets[:, q * PIECE // 16 : (q + 1) * PIECE // 16]
+
+        def g(t, q):
+            dst = grouped[q][:].rearrange("p (j t) -> p j t", t=4)[:, :, t]
+            if t < 2:
+                nc.vector.tensor_copy(dst, raw_v[:, t, :].indirect(cols(q)))
+            else:
+                nc.scalar.activation(dst, xb[:, t - 2, :].indirect(cols(q)), COPY)
+
+        def wi(eng, q):
+            wdst = wgrouped[q][:].rearrange("p (e n j) -> p e n j", e=EPP, j=4)
+            wsrc = wraw[q][:].rearrange("p e (j n) -> p e n j", j=4)
+            if eng == "v":
+                nc.vector.tensor_copy(out=wdst, in_=wsrc)
+            else:
+                nc.scalar.copy(out=wdst, in_=wsrc)
+
+        def qw(q):
+            nc.vector.quantize_mx(out=wcodes[q][:].bitcast(FP8X4), scales=wscales[q][:], in_=wgrouped[q][:])
+
+        def qx(q):
+            nc.vector.quantize_mx(out=xcodes[q][:].bitcast(FP8X4), scales=xscales[q][:], in_=grouped[q][:])
+
+        def mm(q):
+            for h in range(EPP):
+                nc.tensor.matmul_mx(
+                    out=acc[q][:, h * C : (h + 1) * C],
+                    lhsT=wcodes[q][:, h * N : (h + 1) * N].bitcast(FP8X4),
+                    lhsT_scale=wscales[q][:, h * N : (h + 1) * N],
+                    rhs=xcodes[q][:, h * C : (h + 1) * C].bitcast(FP8X4),
+                    rhs_scale=xscales[q][:, h * C : (h + 1) * C],
+                    start=True,
+                    stop=True,
+                )
+
+        def po(eng, q):
+            if eng == "v":
+                nc.vector.tensor_copy(out=sums[q][:], in_=acc[q][:])
+            else:
+                nc.scalar.copy(out=sums[q][:], in_=acc[q][:])
+
+        def sc(q):
+            nc.vector.tensor_tensor(
+                window[:].indirect(cols(q)), sums[q][:], gate_sb[:, q * PIECE : (q + 1) * PIECE], MULT
+            )
+
+        cast()
+        g(0, 0)
+        g(0, 1)
+        g(0, 2)
+        g(0, 3)
+        g(1, 0)
+        g(1, 1)
+        g(1, 2)
+        g(1, 3)
+        g(2, 0)
+        g(3, 0)
+        g(2, 1)
+        g(3, 1)
+        g(2, 2)
+        g(3, 2)
+        g(2, 3)
+        g(3, 3)
+        wi("v", 0)
+        qw(0)
+        qx(0)
+        mm(0)
+        po("v", 0)
+        wi("v", 1)
+        qw(1)
+        qx(1)
+        mm(1)
+        po("v", 1)
+        wi("v", 2)
+        qw(2)
+        qx(2)
+        mm(2)
+        po("s", 2)
+        wi("s", 3)
+        qw(3)
+        qx(3)
+        mm(3)
+        po("s", 3)
+        sc(0)
+        sc(1)
+        sc(2)
+        sc(3)
+        nc.sync.dma_start(out, window[:])

@@ -15,7 +15,7 @@ MULT = mybir.AluOpType.mult
 COPY = mybir.ActivationFunctionType.Copy
 
 P = 128
-CH = 512
+CH = 1024
 NCH = T // CH
 PIECE = 512
 NP = E * C // PIECE
@@ -35,7 +35,7 @@ def tile_routed_moe_kernel(tc, xT, w, gate, offs, out):
         raw_v = keep.tile([P, 2, T], F32, name="raw_v")
         raw_s = [keep.tile([P, 2, CH], F32, name="raw_s%d" % c) for c in range(NCH)]
         wv = w.rearrange("e (p j) n -> p e (j n)", j=4)
-        wraw = [keep.tile([P, EPP, 4 * N], F32, name="wraw%d" % q) for q in range(NP)]
+        wraw = [keep.tile([P, 2 * EPP, 4 * N], F32, name="wraw%d" % c) for c in range(NP // 2)]
         gate_sb = keep.tile([P, E * C], F32, name="gate_sb")
 
         def load_v(t):
@@ -46,15 +46,13 @@ def tile_routed_moe_kernel(tc, xT, w, gate, offs, out):
                 nc.sync.dma_start(raw_s[c][:], xv[:, 2:4, c * CH : (c + 1) * CH])
 
         def load_w(q):
-            nc.sync.dma_start(wraw[q][:], wv[:, q * EPP : (q + 1) * EPP, :])
+            nc.sync.dma_start(wraw[q][:], wv[:, q * 2 * EPP : (q + 1) * 2 * EPP, :])
 
         load_v(0)
         load_v(1)
         load_s()
         load_w(0)
         load_w(1)
-        load_w(2)
-        load_w(3)
         nc.sync.dma_start(gate_sb[:], gate)
 
         xb = keep.tile([P, 2, T], BF16, name="xb")
@@ -84,7 +82,7 @@ def tile_routed_moe_kernel(tc, xT, w, gate, offs, out):
 
         def wi(eng, q):
             wdst = wgrouped[q][:].rearrange("p (e n j) -> p e n j", e=EPP, j=4)
-            wsrc = wraw[q][:].rearrange("p e (j n) -> p e n j", j=4)
+            wsrc = wraw[q // 2][:, (q % 2) * EPP : (q % 2 + 1) * EPP, :].rearrange("p e (j n) -> p e n j", j=4)
             if eng == "v":
                 nc.vector.tensor_copy(out=wdst, in_=wsrc)
             else:
@@ -130,34 +128,34 @@ def tile_routed_moe_kernel(tc, xT, w, gate, offs, out):
         g(1, 3)
         g(2, 0)
         g(3, 0)
-        g(2, 1)
-        g(3, 1)
-        g(2, 2)
-        g(3, 2)
-        g(2, 3)
-        g(3, 3)
         wi("v", 0)
         qw(0)
         qx(0)
         mm(0)
-        po("v", 0)
+        g(2, 1)
+        g(3, 1)
         wi("v", 1)
         qw(1)
+        po("v", 0)
         qx(1)
         mm(1)
+        sc(0)
+        g(2, 2)
         po("v", 1)
+        g(3, 2)
         wi("v", 2)
         qw(2)
         qx(2)
         mm(2)
+        sc(1)
+        g(2, 3)
         po("s", 2)
+        g(3, 3)
         wi("s", 3)
         qw(3)
         qx(3)
         mm(3)
-        po("s", 3)
-        sc(0)
-        sc(1)
         sc(2)
+        po("s", 3)
         sc(3)
         nc.sync.dma_start(out, window[:])

@@ -15,11 +15,13 @@ MULT = mybir.AluOpType.mult
 COPY = mybir.ActivationFunctionType.Copy
 
 P = 128
-CH = 1024
-NCH = T // CH
+PACK = 4
 PIECE = 512
-NP = E * C // PIECE
-EPP = PIECE // C
+PIECES = E * C // PIECE
+EXPERTS = PIECE // C
+HALF = T // 2
+WEIGHT_PIECES_ON_VECTOR = 3
+BANKS_ON_VECTOR = 2
 
 
 def tile_routed_moe_kernel(tc, xT, w, gate, offs, out):
@@ -31,131 +33,96 @@ def tile_routed_moe_kernel(tc, xT, w, gate, offs, out):
         offsets = keep.tile([P, E * C // 16], U16, name="offsets")
         nc.sync.dma_start(offsets[:], offs)
 
-        xv = xT.rearrange("(p t) n -> p t n", t=4)
-        raw_v = keep.tile([P, 2, T], F32, name="raw_v")
-        raw_s = [keep.tile([P, 2, CH], F32, name="raw_s%d" % c) for c in range(NCH)]
-        wv = w.rearrange("e (p j) n -> p e (j n)", j=4)
-        wraw = [keep.tile([P, 2 * EPP, 4 * N], F32, name="wraw%d" % c) for c in range(NP // 2)]
+        planes = xT.rearrange("(p t) n -> p t n", t=PACK)
+        raw01 = keep.tile([P, 2, T], F32, name="raw01")
+        raw23 = [keep.tile([P, 2, HALF], F32, name="raw23_%d" % h) for h in range(2)]
+        w_rows = w.rearrange("e (p t) n -> p e (t n)", t=PACK)
+        wraw = [keep.tile([P, 2 * EXPERTS, PACK * N], F32, name="wraw%d" % h) for h in range(2)]
         gate_sb = keep.tile([P, E * C], F32, name="gate_sb")
-
-        def load_v(t):
-            nc.sync.dma_start(raw_v[:, t, :], xv[:, t, :])
-
-        def load_s():
-            for c in range(NCH):
-                nc.sync.dma_start(raw_s[c][:], xv[:, 2:4, c * CH : (c + 1) * CH])
-
-        def load_w(q):
-            nc.sync.dma_start(wraw[q][:], wv[:, q * 2 * EPP : (q + 1) * 2 * EPP, :])
-
-        load_v(0)
-        load_v(1)
-        load_s()
-        load_w(0)
-        load_w(1)
+        for t in range(2):
+            nc.sync.dma_start(raw01[:, t, :], planes[:, t, :])
+        for h in range(2):
+            nc.sync.dma_start(raw23[h][:], planes[:, 2:4, h * HALF : (h + 1) * HALF])
+        for h in range(2):
+            nc.sync.dma_start(wraw[h][:], w_rows[:, h * 2 * EXPERTS : (h + 1) * 2 * EXPERTS, :])
         nc.sync.dma_start(gate_sb[:], gate)
 
-        xb = keep.tile([P, 2, T], BF16, name="xb")
-        grouped = [keep.tile([P, 4 * PIECE], BF16, name="grouped%d" % q, align_bytes=64) for q in range(NP)]
-        wgrouped = [keep.tile([P, EPP * 4 * N], BF16, name="wgrouped%d" % q, align_bytes=64) for q in range(NP)]
-        wcodes = [keep.tile([P, EPP * N], U32, name="wcodes%d" % q, align_bytes=64) for q in range(NP)]
-        wscales = [keep.tile([P, EPP * N], U8, name="wscales%d" % q, align_bytes=64) for q in range(NP)]
-        xcodes = [keep.tile([P, PIECE], U32, name="xcodes%d" % q, align_bytes=64) for q in range(NP)]
-        xscales = [keep.tile([P, PIECE], U8, name="xscales%d" % q, align_bytes=64) for q in range(NP)]
-        acc = [psum.tile([P, PIECE], F32, name="acc%d" % q) for q in range(NP)]
-        sums = [keep.tile([P, PIECE], F32, name="sums%d" % q) for q in range(NP)]
-        window = keep.tile([P, T], F32, name="window")
+        bf23 = keep.tile([P, 2, T], BF16, name="bf23")
+        grouped = [keep.tile([P, PACK * PIECE], BF16, name="grouped%d" % q, align_bytes=64) for q in range(PIECES)]
+        wgrouped = [keep.tile([P, PACK * EXPERTS * N], BF16, name="wgrouped%d" % q, align_bytes=64) for q in range(PIECES)]
+        wcodes = [keep.tile([P, EXPERTS * N], U32, name="wcodes%d" % q, align_bytes=64) for q in range(PIECES)]
+        wscales = [keep.tile([P, EXPERTS * N], U8, name="wscales%d" % q, align_bytes=64) for q in range(PIECES)]
+        xcodes = [keep.tile([P, PIECE], U32, name="xcodes%d" % q, align_bytes=64) for q in range(PIECES)]
+        xscales = [keep.tile([P, PIECE], U8, name="xscales%d" % q, align_bytes=64) for q in range(PIECES)]
+        bank = [psum.tile([P, PIECE], F32, name="bank%d" % q) for q in range(PIECES)]
+        sums = [keep.tile([P, PIECE], F32, name="sums%d" % q) for q in range(PIECES)]
+        scattered = keep.tile([P, T], F32, name="scattered")
 
-        def cast():
-            for c in range(NCH):
-                nc.scalar.copy(out=xb[:, :, c * CH : (c + 1) * CH], in_=raw_s[c][:])
-
-        def cols(q):
+        def list_piece(q):
             return offsets[:, q * PIECE // 16 : (q + 1) * PIECE // 16]
 
-        def g(t, q):
-            dst = grouped[q][:].rearrange("p (j t) -> p j t", t=4)[:, :, t]
+        def gather(t, q):
+            dst = grouped[q][:].rearrange("p (j t) -> p j t", t=PACK)[:, :, t]
             if t < 2:
-                nc.vector.tensor_copy(dst, raw_v[:, t, :].indirect(cols(q)))
+                nc.vector.tensor_copy(dst, raw01[:, t, :].indirect(list_piece(q)))
             else:
-                nc.scalar.activation(dst, xb[:, t - 2, :].indirect(cols(q)), COPY)
+                nc.scalar.activation(dst, bf23[:, t - 2, :].indirect(list_piece(q)), COPY)
 
-        def wi(eng, q):
-            wdst = wgrouped[q][:].rearrange("p (e n j) -> p e n j", e=EPP, j=4)
-            wsrc = wraw[q // 2][:, (q % 2) * EPP : (q % 2 + 1) * EPP, :].rearrange("p e (j n) -> p e n j", j=4)
-            if eng == "v":
-                nc.vector.tensor_copy(out=wdst, in_=wsrc)
+        def interleave_weights(q):
+            dst = wgrouped[q][:].rearrange("p (e n t) -> p e n t", e=EXPERTS, t=PACK)
+            first = (q % 2) * EXPERTS
+            src = wraw[q // 2][:, first : first + EXPERTS, :].rearrange("p e (t n) -> p e n t", t=PACK)
+            if q < WEIGHT_PIECES_ON_VECTOR:
+                nc.vector.tensor_copy(out=dst, in_=src)
             else:
-                nc.scalar.copy(out=wdst, in_=wsrc)
+                nc.scalar.copy(out=dst, in_=src)
 
-        def qw(q):
+        def quantise_weights(q):
             nc.vector.quantize_mx(out=wcodes[q][:].bitcast(FP8X4), scales=wscales[q][:], in_=wgrouped[q][:])
 
-        def qx(q):
+        def quantise_tokens(q):
             nc.vector.quantize_mx(out=xcodes[q][:].bitcast(FP8X4), scales=xscales[q][:], in_=grouped[q][:])
 
-        def mm(q):
-            for h in range(EPP):
+        def multiply(q):
+            for e in range(EXPERTS):
                 nc.tensor.matmul_mx(
-                    out=acc[q][:, h * C : (h + 1) * C],
-                    lhsT=wcodes[q][:, h * N : (h + 1) * N].bitcast(FP8X4),
-                    lhsT_scale=wscales[q][:, h * N : (h + 1) * N],
-                    rhs=xcodes[q][:, h * C : (h + 1) * C].bitcast(FP8X4),
-                    rhs_scale=xscales[q][:, h * C : (h + 1) * C],
+                    out=bank[q][:, e * C : (e + 1) * C],
+                    lhsT=wcodes[q][:, e * N : (e + 1) * N].bitcast(FP8X4),
+                    lhsT_scale=wscales[q][:, e * N : (e + 1) * N],
+                    rhs=xcodes[q][:, e * C : (e + 1) * C].bitcast(FP8X4),
+                    rhs_scale=xscales[q][:, e * C : (e + 1) * C],
                     start=True,
                     stop=True,
                 )
 
-        def po(eng, q):
-            if eng == "v":
-                nc.vector.tensor_copy(out=sums[q][:], in_=acc[q][:])
+        def empty_bank(q):
+            if q < BANKS_ON_VECTOR:
+                nc.vector.tensor_copy(out=sums[q][:], in_=bank[q][:])
             else:
-                nc.scalar.copy(out=sums[q][:], in_=acc[q][:])
+                nc.scalar.copy(out=sums[q][:], in_=bank[q][:])
 
-        def sc(q):
+        def scatter(q):
             nc.vector.tensor_tensor(
-                window[:].indirect(cols(q)), sums[q][:], gate_sb[:, q * PIECE : (q + 1) * PIECE], MULT
+                scattered[:].indirect(list_piece(q)), sums[q][:], gate_sb[:, q * PIECE : (q + 1) * PIECE], MULT
             )
 
-        cast()
-        g(0, 0)
-        g(0, 1)
-        g(0, 2)
-        g(0, 3)
-        g(1, 0)
-        g(1, 1)
-        g(1, 2)
-        g(1, 3)
-        g(2, 0)
-        g(3, 0)
-        wi("v", 0)
-        qw(0)
-        qx(0)
-        mm(0)
-        g(2, 1)
-        g(3, 1)
-        wi("v", 1)
-        qw(1)
-        po("v", 0)
-        qx(1)
-        mm(1)
-        sc(0)
-        g(2, 2)
-        po("v", 1)
-        g(3, 2)
-        wi("v", 2)
-        qw(2)
-        qx(2)
-        mm(2)
-        sc(1)
-        g(2, 3)
-        po("s", 2)
-        g(3, 3)
-        wi("s", 3)
-        qw(3)
-        qx(3)
-        mm(3)
-        sc(2)
-        po("s", 3)
-        sc(3)
-        nc.sync.dma_start(out, window[:])
+        for h in range(2):
+            nc.scalar.copy(out=bf23[:, :, h * HALF : (h + 1) * HALF], in_=raw23[h][:])
+        for t in range(2):
+            for q in range(PIECES):
+                gather(t, q)
+        for q in range(PIECES):
+            gather(2, q)
+            gather(3, q)
+            interleave_weights(q)
+            quantise_weights(q)
+            if q > 0:
+                empty_bank(q - 1)
+            quantise_tokens(q)
+            multiply(q)
+            if q > 0:
+                scatter(q - 1)
+        empty_bank(PIECES - 1)
+        scatter(PIECES - 1)
+
+        nc.sync.dma_start(out, scattered[:])

@@ -20,7 +20,7 @@ PIECE = 512
 PIECES = E * C // PIECE
 EXPERTS = PIECE // C
 HALF = T // 2
-WEIGHT_PIECES_ON_VECTOR = 3
+PAIRS = PIECES // 2
 BANKS_ON_VECTOR = 2
 
 
@@ -48,10 +48,10 @@ def tile_routed_moe_kernel(tc, xT, w, gate, offs, out):
         nc.sync.dma_start(gate_sb[:], gate)
 
         bf23 = keep.tile([P, 2, T], BF16, name="bf23")
-        grouped = [keep.tile([P, PACK * PIECE], BF16, name="grouped%d" % q, align_bytes=64) for q in range(PIECES)]
-        wgrouped = [keep.tile([P, PACK * EXPERTS * N], BF16, name="wgrouped%d" % q, align_bytes=64) for q in range(PIECES)]
-        wcodes = [keep.tile([P, EXPERTS * N], U32, name="wcodes%d" % q, align_bytes=64) for q in range(PIECES)]
-        wscales = [keep.tile([P, EXPERTS * N], U8, name="wscales%d" % q, align_bytes=64) for q in range(PIECES)]
+        grouped = [keep.tile([P, 2 * PACK * PIECE], BF16, name="grouped%d" % h, align_bytes=64) for h in range(PAIRS)]
+        wgrouped = [keep.tile([P, 2 * PACK * EXPERTS * N], BF16, name="wgrouped%d" % h, align_bytes=64) for h in range(PAIRS)]
+        wcodes = [keep.tile([P, 2 * EXPERTS * N], U32, name="wcodes%d" % h, align_bytes=64) for h in range(PAIRS)]
+        wscales = [keep.tile([P, 2 * EXPERTS * N], U8, name="wscales%d" % h, align_bytes=64) for h in range(PAIRS)]
         xcodes = [keep.tile([P, PIECE], U32, name="xcodes%d" % q, align_bytes=64) for q in range(PIECES)]
         xscales = [keep.tile([P, PIECE], U8, name="xscales%d" % q, align_bytes=64) for q in range(PIECES)]
         bank = [psum.tile([P, PIECE], F32, name="bank%d" % q) for q in range(PIECES)]
@@ -61,34 +61,37 @@ def tile_routed_moe_kernel(tc, xT, w, gate, offs, out):
         def list_piece(q):
             return offsets[:, q * PIECE // 16 : (q + 1) * PIECE // 16]
 
-        def gather(t, q):
-            dst = grouped[q][:].rearrange("p (j t) -> p j t", t=PACK)[:, :, t]
-            if t < 2:
-                nc.vector.tensor_copy(dst, raw01[:, t, :].indirect(list_piece(q)))
-            else:
-                nc.scalar.activation(dst, bf23[:, t - 2, :].indirect(list_piece(q)), COPY)
+        def gather_on_vector(t, h):
+            dst = grouped[h][:].rearrange("p (j t) -> p j t", t=PACK)[:, :, t]
+            entries = offsets[:, h * 2 * PIECE // 16 : (h + 1) * 2 * PIECE // 16]
+            nc.vector.tensor_copy(dst, raw01[:, t, :].indirect(entries))
 
-        def interleave_weights(q):
-            dst = wgrouped[q][:].rearrange("p (e n t) -> p e n t", e=EXPERTS, t=PACK)
-            first = (q % 2) * EXPERTS
-            src = wraw[q // 2][:, first : first + EXPERTS, :].rearrange("p e (t n) -> p e n t", t=PACK)
-            if q < WEIGHT_PIECES_ON_VECTOR:
-                nc.vector.tensor_copy(out=dst, in_=src)
-            else:
-                nc.scalar.copy(out=dst, in_=src)
+        def grouped_piece(q):
+            return grouped[q // 2][:, (q % 2) * PACK * PIECE : (q % 2 + 1) * PACK * PIECE]
 
-        def quantise_weights(q):
-            nc.vector.quantize_mx(out=wcodes[q][:].bitcast(FP8X4), scales=wscales[q][:], in_=wgrouped[q][:])
+        def gather_on_scalar(t, q):
+            dst = grouped_piece(q).rearrange("p (j t) -> p j t", t=PACK)[:, :, t]
+            nc.scalar.activation(dst, bf23[:, t - 2, :].indirect(list_piece(q)), COPY)
+
+        def interleave_weights(h):
+            nc.vector.tensor_copy(
+                out=wgrouped[h][:].rearrange("p (e n t) -> p e n t", e=2 * EXPERTS, t=PACK),
+                in_=wraw[h][:].rearrange("p e (t n) -> p e n t", t=PACK),
+            )
+
+        def quantise_weights(h):
+            nc.vector.quantize_mx(out=wcodes[h][:].bitcast(FP8X4), scales=wscales[h][:], in_=wgrouped[h][:])
 
         def quantise_tokens(q):
-            nc.vector.quantize_mx(out=xcodes[q][:].bitcast(FP8X4), scales=xscales[q][:], in_=grouped[q][:])
+            nc.vector.quantize_mx(out=xcodes[q][:].bitcast(FP8X4), scales=xscales[q][:], in_=grouped_piece(q))
 
         def multiply(q):
             for e in range(EXPERTS):
+                mine = slice(((q % 2) * EXPERTS + e) * N, ((q % 2) * EXPERTS + e + 1) * N)
                 nc.tensor.matmul_mx(
                     out=bank[q][:, e * C : (e + 1) * C],
-                    lhsT=wcodes[q][:, e * N : (e + 1) * N].bitcast(FP8X4),
-                    lhsT_scale=wscales[q][:, e * N : (e + 1) * N],
+                    lhsT=wcodes[q // 2][:, mine].bitcast(FP8X4),
+                    lhsT_scale=wscales[q // 2][:, mine],
                     rhs=xcodes[q][:, e * C : (e + 1) * C].bitcast(FP8X4),
                     rhs_scale=xscales[q][:, e * C : (e + 1) * C],
                     start=True,
@@ -109,13 +112,14 @@ def tile_routed_moe_kernel(tc, xT, w, gate, offs, out):
         for h in range(2):
             nc.scalar.copy(out=bf23[:, :, h * HALF : (h + 1) * HALF], in_=raw23[h][:])
         for t in range(2):
-            for q in range(PIECES):
-                gather(t, q)
+            for h in range(PAIRS):
+                gather_on_vector(t, h)
         for q in range(PIECES):
-            gather(2, q)
-            gather(3, q)
-            interleave_weights(q)
-            quantise_weights(q)
+            gather_on_scalar(2, q)
+            gather_on_scalar(3, q)
+            if q % 2 == 0:
+                interleave_weights(q // 2)
+                quantise_weights(q // 2)
             if q > 0:
                 empty_bank(q - 1)
             quantise_tokens(q)

@@ -20,7 +20,7 @@ PIECE = 512
 PIECES = E * C // PIECE
 EXPERTS = PIECE // C
 HALF = T // 2
-PAIRS = PIECES // 2
+WEIGHT_PIECES_ON_VECTOR = 3
 BANKS_ON_VECTOR = 2
 
 
@@ -34,13 +34,13 @@ def tile_routed_moe_kernel(tc, xT, w, gate, offs, out):
         nc.sync.dma_start(offsets[:], offs)
 
         planes = xT.rearrange("(p t) n -> p t n", t=PACK)
-        raw01 = keep.tile([P, 2, T], F32, name="raw01")
+        raw01 = [keep.tile([P, T], F32, name="raw%d" % t) for t in range(2)]
         raw23 = [keep.tile([P, 2, HALF], F32, name="raw23_%d" % h) for h in range(2)]
         w_rows = w.rearrange("e (p t) n -> p e (t n)", t=PACK)
         wraw = [keep.tile([P, 2 * EXPERTS, PACK * N], F32, name="wraw%d" % h) for h in range(2)]
         gate_sb = keep.tile([P, E * C], F32, name="gate_sb")
         for t in range(2):
-            nc.sync.dma_start(raw01[:, t, :], planes[:, t, :])
+            nc.sync.dma_start(raw01[t][:], planes[:, t, :])
         for h in range(2):
             nc.sync.dma_start(raw23[h][:], planes[:, 2:4, h * HALF : (h + 1) * HALF])
         for h in range(2):
@@ -48,10 +48,11 @@ def tile_routed_moe_kernel(tc, xT, w, gate, offs, out):
         nc.sync.dma_start(gate_sb[:], gate)
 
         bf23 = keep.tile([P, 2, T], BF16, name="bf23")
-        grouped = [keep.tile([P, 2 * PACK * PIECE], BF16, name="grouped%d" % h, align_bytes=64) for h in range(PAIRS)]
-        wgrouped = [keep.tile([P, 2 * PACK * EXPERTS * N], BF16, name="wgrouped%d" % h, align_bytes=64) for h in range(PAIRS)]
-        wcodes = [keep.tile([P, 2 * EXPERTS * N], U32, name="wcodes%d" % h, align_bytes=64) for h in range(PAIRS)]
-        wscales = [keep.tile([P, 2 * EXPERTS * N], U8, name="wscales%d" % h, align_bytes=64) for h in range(PAIRS)]
+        got = [keep.tile([P, 2, PIECE], F32, name="got%d" % q) for q in range(PIECES)]
+        grouped = [keep.tile([P, PACK * PIECE], BF16, name="grouped%d" % q, align_bytes=64) for q in range(PIECES)]
+        wgrouped = [keep.tile([P, PACK * EXPERTS * N], BF16, name="wgrouped%d" % q, align_bytes=64) for q in range(PIECES)]
+        wcodes = [keep.tile([P, EXPERTS * N], U32, name="wcodes%d" % q, align_bytes=64) for q in range(PIECES)]
+        wscales = [keep.tile([P, EXPERTS * N], U8, name="wscales%d" % q, align_bytes=64) for q in range(PIECES)]
         xcodes = [keep.tile([P, PIECE], U32, name="xcodes%d" % q, align_bytes=64) for q in range(PIECES)]
         xscales = [keep.tile([P, PIECE], U8, name="xscales%d" % q, align_bytes=64) for q in range(PIECES)]
         bank = [psum.tile([P, PIECE], F32, name="bank%d" % q) for q in range(PIECES)]
@@ -61,37 +62,34 @@ def tile_routed_moe_kernel(tc, xT, w, gate, offs, out):
         def list_piece(q):
             return offsets[:, q * PIECE // 16 : (q + 1) * PIECE // 16]
 
-        def gather_on_vector(t, h):
-            dst = grouped[h][:].rearrange("p (j t) -> p j t", t=PACK)[:, :, t]
-            entries = offsets[:, h * 2 * PIECE // 16 : (h + 1) * 2 * PIECE // 16]
-            nc.vector.tensor_copy(dst, raw01[:, t, :].indirect(entries))
+        def gather(t, q):
+            dst = grouped[q][:].rearrange("p (j t) -> p j t", t=PACK)[:, :, t]
+            if t < 2:
+                nc.vector.tensor_copy(got[q][:, t, :], raw01[t][:].indirect(list_piece(q)))
+            else:
+                nc.scalar.activation(dst, bf23[:, t - 2, :].indirect(list_piece(q)), COPY)
 
-        def grouped_piece(q):
-            return grouped[q // 2][:, (q % 2) * PACK * PIECE : (q % 2 + 1) * PACK * PIECE]
+        def interleave_weights(q):
+            dst = wgrouped[q][:].rearrange("p (e n t) -> p e n t", e=EXPERTS, t=PACK)
+            first = (q % 2) * EXPERTS
+            src = wraw[q // 2][:, first : first + EXPERTS, :].rearrange("p e (t n) -> p e n t", t=PACK)
+            if q < WEIGHT_PIECES_ON_VECTOR:
+                nc.vector.tensor_copy(out=dst, in_=src)
+            else:
+                nc.scalar.copy(out=dst, in_=src)
 
-        def gather_on_scalar(t, q):
-            dst = grouped_piece(q).rearrange("p (j t) -> p j t", t=PACK)[:, :, t]
-            nc.scalar.activation(dst, bf23[:, t - 2, :].indirect(list_piece(q)), COPY)
-
-        def interleave_weights(h):
-            nc.vector.tensor_copy(
-                out=wgrouped[h][:].rearrange("p (e n t) -> p e n t", e=2 * EXPERTS, t=PACK),
-                in_=wraw[h][:].rearrange("p e (t n) -> p e n t", t=PACK),
-            )
-
-        def quantise_weights(h):
-            nc.vector.quantize_mx(out=wcodes[h][:].bitcast(FP8X4), scales=wscales[h][:], in_=wgrouped[h][:])
+        def quantise_weights(q):
+            nc.vector.quantize_mx(out=wcodes[q][:].bitcast(FP8X4), scales=wscales[q][:], in_=wgrouped[q][:])
 
         def quantise_tokens(q):
-            nc.vector.quantize_mx(out=xcodes[q][:].bitcast(FP8X4), scales=xscales[q][:], in_=grouped_piece(q))
+            nc.vector.quantize_mx(out=xcodes[q][:].bitcast(FP8X4), scales=xscales[q][:], in_=grouped[q][:])
 
         def multiply(q):
             for e in range(EXPERTS):
-                mine = slice(((q % 2) * EXPERTS + e) * N, ((q % 2) * EXPERTS + e + 1) * N)
                 nc.tensor.matmul_mx(
                     out=bank[q][:, e * C : (e + 1) * C],
-                    lhsT=wcodes[q // 2][:, mine].bitcast(FP8X4),
-                    lhsT_scale=wscales[q // 2][:, mine],
+                    lhsT=wcodes[q][:, e * N : (e + 1) * N].bitcast(FP8X4),
+                    lhsT_scale=wscales[q][:, e * N : (e + 1) * N],
                     rhs=xcodes[q][:, e * C : (e + 1) * C].bitcast(FP8X4),
                     rhs_scale=xscales[q][:, e * C : (e + 1) * C],
                     start=True,
@@ -112,14 +110,18 @@ def tile_routed_moe_kernel(tc, xT, w, gate, offs, out):
         for h in range(2):
             nc.scalar.copy(out=bf23[:, :, h * HALF : (h + 1) * HALF], in_=raw23[h][:])
         for t in range(2):
-            for h in range(PAIRS):
-                gather_on_vector(t, h)
+            for q in range(PIECES):
+                gather(t, q)
         for q in range(PIECES):
-            gather_on_scalar(2, q)
-            gather_on_scalar(3, q)
-            if q % 2 == 0:
-                interleave_weights(q // 2)
-                quantise_weights(q // 2)
+            nc.vector.tensor_copy(
+                out=grouped[q][:].rearrange("p (j t) -> p j t", t=PACK)[:, :, 0:2],
+                in_=got[q][:].rearrange("p t j -> p j t"),
+            )
+        for q in range(PIECES):
+            gather(2, q)
+            gather(3, q)
+            interleave_weights(q)
+            quantise_weights(q)
             if q > 0:
                 empty_bank(q - 1)
             quantise_tokens(q)

@@ -19,7 +19,9 @@ PACK = 4
 PIECE = 512
 PIECES = E * C // PIECE
 EXPERTS = PIECE // C
-HALF = T // 2
+AHEAD = 2
+WIDE = AHEAD * PIECE
+ROUNDINGS_ON_VECTOR = 1
 WEIGHT_PIECES_ON_VECTOR = 3
 BANKS_ON_VECTOR = 2
 
@@ -34,42 +36,60 @@ def tile_routed_moe_kernel(tc, xT, w, gate, offs, out):
         nc.sync.dma_start(offsets[:], offs)
 
         planes = xT.rearrange("(p t) n -> p t n", t=PACK)
-        raw01 = [keep.tile([P, T], F32, name="raw%d" % t) for t in range(2)]
-        raw23 = [keep.tile([P, 2, HALF], F32, name="raw23_%d" % h) for h in range(2)]
+        raw = [keep.tile([P, T], F32, name="raw%d" % t, align_bytes=64) for t in range(PACK)]
         w_rows = w.rearrange("e (p t) n -> p e (t n)", t=PACK)
         wraw = [keep.tile([P, 2 * EXPERTS, PACK * N], F32, name="wraw%d" % h) for h in range(2)]
         gate_sb = keep.tile([P, E * C], F32, name="gate_sb")
-        for t in range(2):
-            nc.sync.dma_start(raw01[t][:], planes[:, t, :])
-        for h in range(2):
-            nc.sync.dma_start(raw23[h][:], planes[:, 2:4, h * HALF : (h + 1) * HALF])
+        for t in (0, 2, 3, 1):
+            nc.sync.dma_start(raw[t][:], planes[:, t, :])
         for h in range(2):
             nc.sync.dma_start(wraw[h][:], w_rows[:, h * 2 * EXPERTS : (h + 1) * 2 * EXPERTS, :])
         nc.sync.dma_start(gate_sb[:], gate)
 
         bf23 = keep.tile([P, 2, T], BF16, name="bf23")
-        got = [keep.tile([P, 2, PIECE], F32, name="got%d" % q) for q in range(PIECES)]
-        grouped = [keep.tile([P, PACK * PIECE], BF16, name="grouped%d" % q, align_bytes=64) for q in range(PIECES)]
-        wgrouped = [keep.tile([P, PACK * EXPERTS * N], BF16, name="wgrouped%d" % q, align_bytes=64) for q in range(PIECES)]
-        wcodes = [keep.tile([P, EXPERTS * N], U32, name="wcodes%d" % q, align_bytes=64) for q in range(PIECES)]
+        got = {}
+        grouped = {}
+        wgrouped = {}
+        wcodes = {}
         wscales = [keep.tile([P, EXPERTS * N], U8, name="wscales%d" % q, align_bytes=64) for q in range(PIECES)]
-        xcodes = [keep.tile([P, PIECE], U32, name="xcodes%d" % q, align_bytes=64) for q in range(PIECES)]
+        xcodes = {}
         xscales = [keep.tile([P, PIECE], U8, name="xscales%d" % q, align_bytes=64) for q in range(PIECES)]
         bank = [psum.tile([P, PIECE], F32, name="bank%d" % q) for q in range(PIECES)]
-        sums = [keep.tile([P, PIECE], F32, name="sums%d" % q) for q in range(PIECES)]
+        sums = {}
         scattered = keep.tile([P, T], F32, name="scattered")
 
         def list_piece(q):
             return offsets[:, q * PIECE // 16 : (q + 1) * PIECE // 16]
 
+        def cast(t):
+            nc.vector.tensor_copy(out=bf23[:, t - 2, :], in_=raw[t][:])
+
+        def gather_wide(t, h):
+            if h not in got:
+                got[h] = keep.tile([P, 2, WIDE], F32, name="got%d" % h, tag="early" if h == 0 else "raw2", align_bytes=64)
+            nc.vector.tensor_copy(got[h][:, t, :], raw[t][:].indirect(offsets[:, h * WIDE // 16 : (h + 1) * WIDE // 16]))
+
         def gather(t, q):
+            if q not in grouped:
+                grouped[q] = keep.tile(
+                    [P, PACK * PIECE], BF16, name="grouped%d" % q, tag=("grouped0", "odd", "early", "odd")[q], align_bytes=64
+                )
             dst = grouped[q][:].rearrange("p (j t) -> p j t", t=PACK)[:, :, t]
-            if t < 2:
-                nc.vector.tensor_copy(got[q][:, t, :], raw01[t][:].indirect(list_piece(q)))
+            nc.scalar.activation(dst, bf23[:, t - 2, :].indirect(list_piece(q)), COPY)
+
+        def round_pair(q):
+            first = (q % AHEAD) * PIECE
+            dst = grouped[q][:].rearrange("p (j t) -> p j t", t=PACK)[:, :, 0:2]
+            src = got[q // AHEAD][:, :, first : first + PIECE].rearrange("p t j -> p j t")
+            if q < ROUNDINGS_ON_VECTOR:
+                nc.vector.tensor_copy(out=dst, in_=src)
             else:
-                nc.scalar.activation(dst, bf23[:, t - 2, :].indirect(list_piece(q)), COPY)
+                nc.scalar.copy(out=dst, in_=src)
 
         def interleave_weights(q):
+            wgrouped[q] = keep.tile(
+                [P, PACK * EXPERTS * N], BF16, name="wgrouped%d" % q, tag=("late1", "late0", "wgrouped2", "wgrouped3")[q], align_bytes=64
+            )
             dst = wgrouped[q][:].rearrange("p (e n t) -> p e n t", e=EXPERTS, t=PACK)
             first = (q % 2) * EXPERTS
             src = wraw[q // 2][:, first : first + EXPERTS, :].rearrange("p e (t n) -> p e n t", t=PACK)
@@ -79,9 +99,11 @@ def tile_routed_moe_kernel(tc, xT, w, gate, offs, out):
                 nc.scalar.copy(out=dst, in_=src)
 
         def quantise_weights(q):
+            wcodes[q] = keep.tile([P, EXPERTS * N], U32, name="wcodes%d" % q, tag="early" if q == PIECES - 1 else "wcodes%d" % q, align_bytes=64)
             nc.vector.quantize_mx(out=wcodes[q][:].bitcast(FP8X4), scales=wscales[q][:], in_=wgrouped[q][:])
 
         def quantise_tokens(q):
+            xcodes[q] = keep.tile([P, PIECE], U32, name="xcodes%d" % q, tag="late%d" % (q % AHEAD), align_bytes=64)
             nc.vector.quantize_mx(out=xcodes[q][:].bitcast(FP8X4), scales=xscales[q][:], in_=grouped[q][:])
 
         def multiply(q):
@@ -97,6 +119,7 @@ def tile_routed_moe_kernel(tc, xT, w, gate, offs, out):
                 )
 
         def empty_bank(q):
+            sums[q] = keep.tile([P, PIECE], F32, name="sums%d" % q, tag="late%d" % (q % AHEAD), align_bytes=64)
             if q < BANKS_ON_VECTOR:
                 nc.vector.tensor_copy(out=sums[q][:], in_=bank[q][:])
             else:
@@ -107,28 +130,35 @@ def tile_routed_moe_kernel(tc, xT, w, gate, offs, out):
                 scattered[:].indirect(list_piece(q)), sums[q][:], gate_sb[:, q * PIECE : (q + 1) * PIECE], MULT
             )
 
-        for h in range(2):
-            nc.scalar.copy(out=bf23[:, :, h * HALF : (h + 1) * HALF], in_=raw23[h][:])
-        for t in range(2):
-            for q in range(PIECES):
+        gather_wide(0, 0)
+        cast(2)
+        gather_wide(0, 1)
+        cast(3)
+        gather_wide(1, 0)
+        gather_wide(1, 1)
+        for t in (2, 3):
+            for q in range(AHEAD):
                 gather(t, q)
-        for q in range(PIECES):
-            nc.vector.tensor_copy(
-                out=grouped[q][:].rearrange("p (j t) -> p j t", t=PACK)[:, :, 0:2],
-                in_=got[q][:].rearrange("p t j -> p j t"),
-            )
-        for q in range(PIECES):
-            gather(2, q)
-            gather(3, q)
+        for q in range(AHEAD):
+            round_pair(q)
+        for q in range(AHEAD):
             interleave_weights(q)
             quantise_weights(q)
-            if q > 0:
-                empty_bank(q - 1)
+        for q in range(AHEAD):
             quantise_tokens(q)
             multiply(q)
-            if q > 0:
-                scatter(q - 1)
-        empty_bank(PIECES - 1)
-        scatter(PIECES - 1)
+        for q in range(AHEAD, PIECES):
+            gather(2, q)
+            gather(3, q)
+            round_pair(q)
+            empty_bank(q - AHEAD)
+            scatter(q - AHEAD)
+            interleave_weights(q)
+            quantise_weights(q)
+            quantise_tokens(q)
+            multiply(q)
+        for q in range(PIECES - AHEAD, PIECES):
+            empty_bank(q)
+            scatter(q)
 
         nc.sync.dma_start(out, scattered[:])

@@ -19,11 +19,12 @@ PACK = 4
 PIECE = 512
 PIECES = E * C // PIECE
 EXPERTS = PIECE // C
+RUN = 4
 AHEAD = 2
 WIDE = AHEAD * PIECE
 ROUNDINGS_ON_VECTOR = 1
 WEIGHT_PIECES_ON_VECTOR = 3
-BANKS_ON_VECTOR = 2
+BANKS_ON_VECTOR = 1
 
 
 def tile_routed_moe_kernel(tc, xT, w, gate, offs, out):
@@ -72,7 +73,7 @@ def tile_routed_moe_kernel(tc, xT, w, gate, offs, out):
         def gather(t, q):
             if q not in grouped:
                 grouped[q] = keep.tile(
-                    [P, PACK * PIECE], BF16, name="grouped%d" % q, tag=("grouped0", "odd", "early", "odd")[q], align_bytes=64
+                    [P, PACK * PIECE], BF16, name="grouped%d" % q, tag=("grouped0", "grouped1", "early", "xscales1")[q], align_bytes=64
                 )
             dst = grouped[q][:].rearrange("p (j t) -> p j t", t=PACK)[:, :, t]
             nc.scalar.activation(dst, bf23[:, t - 2, :].indirect(list_piece(q)), COPY)
@@ -90,9 +91,9 @@ def tile_routed_moe_kernel(tc, xT, w, gate, offs, out):
             wgrouped[q] = keep.tile(
                 [P, PACK * EXPERTS * N], BF16, name="wgrouped%d" % q, tag=("late1", "late0", "wgrouped2", "wgrouped3")[q], align_bytes=64
             )
-            dst = wgrouped[q][:].rearrange("p (e n t) -> p e n t", e=EXPERTS, t=PACK)
+            dst = wgrouped[q][:].rearrange("p (e c i t) -> p e c t i", e=EXPERTS, i=RUN, t=PACK)
             first = (q % 2) * EXPERTS
-            src = wraw[q // 2][:, first : first + EXPERTS, :].rearrange("p e (t n) -> p e n t", t=PACK)
+            src = wraw[q // 2][:, first : first + EXPERTS, :].rearrange("p e (t c i) -> p e c t i", t=PACK, i=RUN)
             if q < WEIGHT_PIECES_ON_VECTOR:
                 nc.vector.tensor_copy(out=dst, in_=src)
             else:
@@ -148,10 +149,10 @@ def tile_routed_moe_kernel(tc, xT, w, gate, offs, out):
             quantise_tokens(q)
             multiply(q)
         for q in range(AHEAD, PIECES):
+            empty_bank(q - AHEAD)
             gather(2, q)
             gather(3, q)
             round_pair(q)
-            empty_bank(q - AHEAD)
             scatter(q - AHEAD)
             interleave_weights(q)
             quantise_weights(q)

@@ -20,11 +20,9 @@ PIECE = 512
 PIECES = E * C // PIECE
 EXPERTS = PIECE // C
 RUN = 4
-AHEAD = 2
-WIDE = AHEAD * PIECE
-ROUNDINGS_ON_VECTOR = 1
-WEIGHT_PIECES_ON_VECTOR = 3
+WIDE = 2 * PIECE
 BANKS_ON_VECTOR = 1
+CAST_ON_SCALAR = 768
 
 
 def tile_routed_moe_kernel(tc, xT, w, gate, offs, out):
@@ -39,7 +37,7 @@ def tile_routed_moe_kernel(tc, xT, w, gate, offs, out):
         planes = xT.rearrange("(p t) n -> p t n", t=PACK)
         raw = [keep.tile([P, T], F32, name="raw%d" % t, align_bytes=64) for t in range(PACK)]
         w_rows = w.rearrange("e (p t) n -> p e (t n)", t=PACK)
-        wraw = [keep.tile([P, 2 * EXPERTS, PACK * N], F32, name="wraw%d" % h) for h in range(2)]
+        wraw = [keep.tile([P, 2 * EXPERTS, PACK * N], F32, name="wraw%d" % h, align_bytes=64) for h in range(2)]
         gate_sb = keep.tile([P, E * C], F32, name="gate_sb")
         for t in (0, 2, 3, 1):
             nc.sync.dma_start(raw[t][:], planes[:, t, :])
@@ -62,50 +60,47 @@ def tile_routed_moe_kernel(tc, xT, w, gate, offs, out):
         def list_piece(q):
             return offsets[:, q * PIECE // 16 : (q + 1) * PIECE // 16]
 
-        def cast(t):
-            nc.vector.tensor_copy(out=bf23[:, t - 2, :], in_=raw[t][:])
-
         def gather_wide(t, h):
             if h not in got:
-                got[h] = keep.tile([P, 2, WIDE], F32, name="got%d" % h, tag="early" if h == 0 else "raw2", align_bytes=64)
+                got[h] = keep.tile([P, 2, WIDE], F32, name="got%d" % h, tag=("got0", "raw2")[h], align_bytes=64)
             nc.vector.tensor_copy(got[h][:, t, :], raw[t][:].indirect(offsets[:, h * WIDE // 16 : (h + 1) * WIDE // 16]))
 
         def gather(t, q):
             if q not in grouped:
                 grouped[q] = keep.tile(
-                    [P, PACK * PIECE], BF16, name="grouped%d" % q, tag=("grouped0", "grouped1", "early", "xscales1")[q], align_bytes=64
+                    [P, PACK * PIECE], BF16, name="grouped%d" % q, tag=("grouped0", "grouped1", "wgrouped0", "xscales1")[q], align_bytes=64
                 )
             dst = grouped[q][:].rearrange("p (j t) -> p j t", t=PACK)[:, :, t]
             nc.scalar.activation(dst, bf23[:, t - 2, :].indirect(list_piece(q)), COPY)
 
         def round_pair(q):
-            first = (q % AHEAD) * PIECE
+            first = (q % 2) * PIECE
             dst = grouped[q][:].rearrange("p (j t) -> p j t", t=PACK)[:, :, 0:2]
-            src = got[q // AHEAD][:, :, first : first + PIECE].rearrange("p t j -> p j t")
-            if q < ROUNDINGS_ON_VECTOR:
-                nc.vector.tensor_copy(out=dst, in_=src)
-            else:
-                nc.scalar.copy(out=dst, in_=src)
+            nc.scalar.copy(out=dst, in_=got[q // 2][:, :, first : first + PIECE].rearrange("p t j -> p j t"))
 
         def interleave_weights(q):
             wgrouped[q] = keep.tile(
-                [P, PACK * EXPERTS * N], BF16, name="wgrouped%d" % q, tag=("late1", "late0", "wgrouped2", "wgrouped3")[q], align_bytes=64
+                [P, PACK * EXPERTS * N], BF16, name="wgrouped%d" % q, align_bytes=64
             )
             dst = wgrouped[q][:].rearrange("p (e c i t) -> p e c t i", e=EXPERTS, i=RUN, t=PACK)
             first = (q % 2) * EXPERTS
             src = wraw[q // 2][:, first : first + EXPERTS, :].rearrange("p e (t c i) -> p e c t i", t=PACK, i=RUN)
-            if q < WEIGHT_PIECES_ON_VECTOR:
-                nc.vector.tensor_copy(out=dst, in_=src)
-            else:
-                nc.scalar.copy(out=dst, in_=src)
+            nc.vector.tensor_copy(out=dst, in_=src)
 
         def quantise_weights(q):
-            wcodes[q] = keep.tile([P, EXPERTS * N], U32, name="wcodes%d" % q, tag="early" if q == PIECES - 1 else "wcodes%d" % q, align_bytes=64)
+            tag = ("wcodes0", "wcodes1", "grouped1", "wgrouped0")[q]
+            wcodes[q] = keep.tile([P, EXPERTS * N], U32, name="wcodes%d" % q, tag=tag, align_bytes=64)
             nc.vector.quantize_mx(out=wcodes[q][:].bitcast(FP8X4), scales=wscales[q][:], in_=wgrouped[q][:])
 
         def quantise_tokens(q):
-            xcodes[q] = keep.tile([P, PIECE], U32, name="xcodes%d" % q, tag="late%d" % (q % AHEAD), align_bytes=64)
-            nc.vector.quantize_mx(out=xcodes[q][:].bitcast(FP8X4), scales=xscales[q][:], in_=grouped[q][:])
+            if q not in xcodes:
+                if q == 0:
+                    pair = keep.tile([P, 2 * PIECE], U32, name="xcodes01", tag="wgrouped1", align_bytes=64)
+                    xcodes[0], xcodes[1] = pair[:, :PIECE], pair[:, PIECE:]
+                else:
+                    single = keep.tile([P, PIECE], U32, name="xcodes%d" % q, tag="late%d" % (q % 2), align_bytes=64)
+                    xcodes[q] = single[:]
+            nc.vector.quantize_mx(out=xcodes[q].bitcast(FP8X4), scales=xscales[q][:], in_=grouped[q][:])
 
         def multiply(q):
             for e in range(EXPERTS):
@@ -120,7 +115,7 @@ def tile_routed_moe_kernel(tc, xT, w, gate, offs, out):
                 )
 
         def empty_bank(q):
-            sums[q] = keep.tile([P, PIECE], F32, name="sums%d" % q, tag="late%d" % (q % AHEAD), align_bytes=64)
+            sums[q] = keep.tile([P, PIECE], F32, name="sums%d" % q, tag="late%d" % (q % 2), align_bytes=64)
             if q < BANKS_ON_VECTOR:
                 nc.vector.tensor_copy(out=sums[q][:], in_=bank[q][:])
             else:
@@ -131,34 +126,45 @@ def tile_routed_moe_kernel(tc, xT, w, gate, offs, out):
                 scattered[:].indirect(list_piece(q)), sums[q][:], gate_sb[:, q * PIECE : (q + 1) * PIECE], MULT
             )
 
+        spare = keep.tile([P, 2], F32, name="spare")
+        nc.gpsimd.memset(spare[:, 0:1], 0.0)
+        nc.scalar.copy(out=spare[:, 1:2], in_=spare[:, 0:1])
         gather_wide(0, 0)
-        cast(2)
+        nc.scalar.copy(out=bf23[:, 0, :CAST_ON_SCALAR], in_=raw[2][:, :CAST_ON_SCALAR])
+        nc.vector.tensor_copy(out=bf23[:, 0, CAST_ON_SCALAR:], in_=raw[2][:, CAST_ON_SCALAR:])
         gather_wide(0, 1)
-        cast(3)
+        nc.vector.tensor_copy(out=bf23[:, 1, :], in_=raw[3][:])
         gather_wide(1, 0)
         gather_wide(1, 1)
         for t in (2, 3):
-            for q in range(AHEAD):
+            for q in range(2):
                 gather(t, q)
-        for q in range(AHEAD):
+        for q in range(2):
             round_pair(q)
-        for q in range(AHEAD):
+        for q in range(2):
             interleave_weights(q)
             quantise_weights(q)
-        for q in range(AHEAD):
-            quantise_tokens(q)
-            multiply(q)
-        for q in range(AHEAD, PIECES):
-            empty_bank(q - AHEAD)
+        quantise_tokens(0)
+        multiply(0)
+        interleave_weights(2)
+        interleave_weights(3)
+        quantise_tokens(1)
+        multiply(1)
+        empty_bank(0)
+        for q in range(2, PIECES):
+            if q > 2:
+                empty_bank(q - 2)
+            else:
+                quantise_weights(q)
             gather(2, q)
             gather(3, q)
             round_pair(q)
-            scatter(q - AHEAD)
-            interleave_weights(q)
-            quantise_weights(q)
+            scatter(q - 2)
+            if q > 2:
+                quantise_weights(q)
             quantise_tokens(q)
             multiply(q)
-        for q in range(PIECES - AHEAD, PIECES):
+        for q in range(PIECES - 2, PIECES):
             empty_bank(q)
             scatter(q)
 

@@ -22,7 +22,10 @@ EXPERTS = PIECE // C
 RUN = 4
 WIDE = 2 * PIECE
 BANKS_ON_VECTOR = 1
-CAST_ON_SCALAR = 768
+PARTS = 2
+PART = T // PARTS
+LAST = PIECES - 1
+LAST_ON_VECTOR = PIECE // 2
 
 
 def tile_routed_moe_kernel(tc, xT, w, gate, offs, out):
@@ -35,11 +38,15 @@ def tile_routed_moe_kernel(tc, xT, w, gate, offs, out):
         nc.sync.dma_start(offsets[:], offs)
 
         planes = xT.rearrange("(p t) n -> p t n", t=PACK)
-        raw = [keep.tile([P, T], F32, name="raw%d" % t, align_bytes=64) for t in range(PACK)]
+        raw = {t: keep.tile([P, T], F32, name="raw%d" % t, align_bytes=64) for t in (0, 1, 3)}
+        raw2 = [keep.tile([P, PART], F32, name="raw2_%d" % c, align_bytes=64) for c in range(PARTS)]
         w_rows = w.rearrange("e (p t) n -> p e (t n)", t=PACK)
         wraw = [keep.tile([P, 2 * EXPERTS, PACK * N], F32, name="wraw%d" % h, align_bytes=64) for h in range(2)]
         gate_sb = keep.tile([P, E * C], F32, name="gate_sb")
-        for t in (0, 2, 3, 1):
+        nc.sync.dma_start(raw[0][:], planes[:, 0, :])
+        for c in range(PARTS):
+            nc.sync.dma_start(raw2[c][:], planes[:, 2, c * PART : (c + 1) * PART])
+        for t in (1, 3):
             nc.sync.dma_start(raw[t][:], planes[:, t, :])
         for h in range(2):
             nc.sync.dma_start(wraw[h][:], w_rows[:, h * 2 * EXPERTS : (h + 1) * 2 * EXPERTS, :])
@@ -62,21 +69,20 @@ def tile_routed_moe_kernel(tc, xT, w, gate, offs, out):
 
         def gather_wide(t, h):
             if h not in got:
-                got[h] = keep.tile([P, 2, WIDE], F32, name="got%d" % h, tag=("got0", "raw2")[h], align_bytes=64)
+                got[h] = keep.tile([P, 2, WIDE], F32, name="got%d" % h, align_bytes=64)
             nc.vector.tensor_copy(got[h][:, t, :], raw[t][:].indirect(offsets[:, h * WIDE // 16 : (h + 1) * WIDE // 16]))
 
         def gather(t, q):
             if q not in grouped:
-                grouped[q] = keep.tile(
-                    [P, PACK * PIECE], BF16, name="grouped%d" % q, tag=("grouped0", "grouped1", "wgrouped0", "xscales1")[q], align_bytes=64
-                )
+                tag = ("grouped0", "grouped1", "wgrouped1", "xscales1")[q]
+                grouped[q] = keep.tile([P, PACK * PIECE], BF16, name="grouped%d" % q, tag=tag, align_bytes=64)
             dst = grouped[q][:].rearrange("p (j t) -> p j t", t=PACK)[:, :, t]
             nc.scalar.activation(dst, bf23[:, t - 2, :].indirect(list_piece(q)), COPY)
 
-        def round_pair(q):
+        def round_pair(copy, q, a, b):
             first = (q % 2) * PIECE
-            dst = grouped[q][:].rearrange("p (j t) -> p j t", t=PACK)[:, :, 0:2]
-            nc.scalar.copy(out=dst, in_=got[q // 2][:, :, first : first + PIECE].rearrange("p t j -> p j t"))
+            dst = grouped[q][:].rearrange("p (j t) -> p j t", t=PACK)[:, a:b, 0:2]
+            copy(out=dst, in_=got[q // 2][:, :, first + a : first + b].rearrange("p t j -> p j t"))
 
         def interleave_weights(q):
             wgrouped[q] = keep.tile(
@@ -88,19 +94,14 @@ def tile_routed_moe_kernel(tc, xT, w, gate, offs, out):
             nc.vector.tensor_copy(out=dst, in_=src)
 
         def quantise_weights(q):
-            tag = ("wcodes0", "wcodes1", "grouped1", "wgrouped0")[q]
+            tag = ("wcodes0", "wcodes1", "grouped1", "wgrouped1")[q]
             wcodes[q] = keep.tile([P, EXPERTS * N], U32, name="wcodes%d" % q, tag=tag, align_bytes=64)
             nc.vector.quantize_mx(out=wcodes[q][:].bitcast(FP8X4), scales=wscales[q][:], in_=wgrouped[q][:])
 
         def quantise_tokens(q):
-            if q not in xcodes:
-                if q == 0:
-                    pair = keep.tile([P, 2 * PIECE], U32, name="xcodes01", tag="wgrouped1", align_bytes=64)
-                    xcodes[0], xcodes[1] = pair[:, :PIECE], pair[:, PIECE:]
-                else:
-                    single = keep.tile([P, PIECE], U32, name="xcodes%d" % q, tag="late%d" % (q % 2), align_bytes=64)
-                    xcodes[q] = single[:]
-            nc.vector.quantize_mx(out=xcodes[q].bitcast(FP8X4), scales=xscales[q][:], in_=grouped[q][:])
+            tag = ("wgrouped0", "wraw1", "late0", "late1")[q]
+            xcodes[q] = keep.tile([P, PIECE], U32, name="xcodes%d" % q, tag=tag, align_bytes=64)
+            nc.vector.quantize_mx(out=xcodes[q][:].bitcast(FP8X4), scales=xscales[q][:], in_=grouped[q][:])
 
         def multiply(q):
             for e in range(EXPERTS):
@@ -129,42 +130,45 @@ def tile_routed_moe_kernel(tc, xT, w, gate, offs, out):
         spare = keep.tile([P, 2], F32, name="spare")
         nc.gpsimd.memset(spare[:, 0:1], 0.0)
         nc.scalar.copy(out=spare[:, 1:2], in_=spare[:, 0:1])
-        gather_wide(0, 0)
-        nc.scalar.copy(out=bf23[:, 0, :CAST_ON_SCALAR], in_=raw[2][:, :CAST_ON_SCALAR])
-        nc.vector.tensor_copy(out=bf23[:, 0, CAST_ON_SCALAR:], in_=raw[2][:, CAST_ON_SCALAR:])
-        gather_wide(0, 1)
+        for c in range(PARTS):
+            nc.scalar.copy(out=bf23[:, 0, c * PART : (c + 1) * PART], in_=raw2[c][:])
+        for t in (0, 1):
+            for h in range(2):
+                gather_wide(t, h)
         nc.vector.tensor_copy(out=bf23[:, 1, :], in_=raw[3][:])
-        gather_wide(1, 0)
-        gather_wide(1, 1)
-        for t in (2, 3):
-            for q in range(2):
-                gather(t, q)
         for q in range(2):
-            round_pair(q)
+            gather(2, q)
+        for q in range(2):
+            round_pair(nc.scalar.copy, q, 0, PIECE)
+        for q in range(2):
+            gather(3, q)
         for q in range(2):
             interleave_weights(q)
             quantise_weights(q)
         quantise_tokens(0)
         multiply(0)
-        interleave_weights(2)
-        interleave_weights(3)
+        for q in range(2, PIECES):
+            interleave_weights(q)
         quantise_tokens(1)
         multiply(1)
         empty_bank(0)
+        quantise_weights(2)
+        gather(2, 2)
+        gather(3, 2)
+        round_pair(nc.scalar.copy, 2, 0, PIECE)
+        scatter(0)
+        quantise_tokens(2)
+        multiply(2)
+        empty_bank(1)
+        gather(2, LAST)
+        gather(3, LAST)
+        round_pair(nc.vector.tensor_copy, LAST, 0, LAST_ON_VECTOR)
+        round_pair(nc.scalar.copy, LAST, LAST_ON_VECTOR, PIECE)
+        scatter(1)
+        quantise_weights(LAST)
+        quantise_tokens(LAST)
+        multiply(LAST)
         for q in range(2, PIECES):
-            if q > 2:
-                empty_bank(q - 2)
-            else:
-                quantise_weights(q)
-            gather(2, q)
-            gather(3, q)
-            round_pair(q)
-            scatter(q - 2)
-            if q > 2:
-                quantise_weights(q)
-            quantise_tokens(q)
-            multiply(q)
-        for q in range(PIECES - 2, PIECES):
             empty_bank(q)
             scatter(q)
 

@@ -16,16 +16,15 @@ COPY = mybir.ActivationFunctionType.Copy
 
 P = 128
 PACK = 4
-PIECE = 512
-PIECES = E * C // PIECE
-EXPERTS = PIECE // C
+BANK = 512
+PAIR = BANK // C
+PAIRS = E // PAIR
+PIECES = ((0, BANK), (BANK, BANK), (2 * BANK, BANK), (3 * BANK, C), (3 * BANK + C, C))
 RUN = 4
-WIDE = 2 * PIECE
-BANKS_ON_VECTOR = 1
+WIDE = 2 * BANK
 PARTS = 2
 PART = T // PARTS
-LAST = PIECES - 1
-LAST_ON_VECTOR = PIECE // 2
+LOAD_PAIRS = 3
 
 
 def tile_routed_moe_kernel(tc, xT, w, gate, offs, out):
@@ -41,15 +40,16 @@ def tile_routed_moe_kernel(tc, xT, w, gate, offs, out):
         raw = {t: keep.tile([P, T], F32, name="raw%d" % t, align_bytes=64) for t in (0, 1, 3)}
         raw2 = [keep.tile([P, PART], F32, name="raw2_%d" % c, align_bytes=64) for c in range(PARTS)]
         w_rows = w.rearrange("e (p t) n -> p e (t n)", t=PACK)
-        wraw = [keep.tile([P, 2 * EXPERTS, PACK * N], F32, name="wraw%d" % h, align_bytes=64) for h in range(2)]
+        wraw0 = keep.tile([P, LOAD_PAIRS * PAIR, PACK * N], F32, name="wraw0", align_bytes=64)
+        wraw1 = keep.tile([P, E - LOAD_PAIRS * PAIR, PACK * N], F32, name="wraw1", align_bytes=64)
         gate_sb = keep.tile([P, E * C], F32, name="gate_sb")
         nc.sync.dma_start(raw[0][:], planes[:, 0, :])
         for c in range(PARTS):
             nc.sync.dma_start(raw2[c][:], planes[:, 2, c * PART : (c + 1) * PART])
         for t in (1, 3):
             nc.sync.dma_start(raw[t][:], planes[:, t, :])
-        for h in range(2):
-            nc.sync.dma_start(wraw[h][:], w_rows[:, h * 2 * EXPERTS : (h + 1) * 2 * EXPERTS, :])
+        nc.sync.dma_start(wraw0[:], w_rows[:, : LOAD_PAIRS * PAIR, :])
+        nc.sync.dma_start(wraw1[:], w_rows[:, LOAD_PAIRS * PAIR :, :])
         nc.sync.dma_start(gate_sb[:], gate)
 
         bf23 = keep.tile([P, 2, T], BF16, name="bf23")
@@ -57,119 +57,142 @@ def tile_routed_moe_kernel(tc, xT, w, gate, offs, out):
         grouped = {}
         wgrouped = {}
         wcodes = {}
-        wscales = [keep.tile([P, EXPERTS * N], U8, name="wscales%d" % q, align_bytes=64) for q in range(PIECES)]
+        wscales = [keep.tile([P, PAIR * N], U8, name="wscales%d" % q, align_bytes=64) for q in range(PAIRS)]
         xcodes = {}
-        xscales = [keep.tile([P, PIECE], U8, name="xscales%d" % q, align_bytes=64) for q in range(PIECES)]
-        bank = [psum.tile([P, PIECE], F32, name="bank%d" % q) for q in range(PIECES)]
+        xscales = [keep.tile([P, PIECES[i][1]], U8, name="xscales%d" % i, align_bytes=64) for i in range(len(PIECES))]
+        bank = [psum.tile([P, PIECES[i][1]], F32, name="bank%d" % i) for i in range(len(PIECES))]
         sums = {}
         scattered = keep.tile([P, T], F32, name="scattered")
 
-        def list_piece(q):
-            return offsets[:, q * PIECE // 16 : (q + 1) * PIECE // 16]
+        TAGS = {
+            "grouped2": "wgrouped1",
+            "wgrouped3": "wscales1",
+            "grouped3": "xscales1",
+            "grouped4": "xscales2",
+            "sums3": "got1",
+            "xcodes0": "wgrouped0",
+            "xcodes1": "wraw0",
+            "wcodes2": "grouped1",
+            "sums0": "late0",
+            "xcodes2": "late0",
+            "sums2": "late0",
+            "sums1": "late1",
+            "xcodes3": "late1",
+        }
+
+        def new(shape, dtype, name):
+            return keep.tile(shape, dtype, name=name, tag=TAGS.get(name, name), align_bytes=64)
+
+        def entries(first, n):
+            return offsets[:, first // 16 : (first + n) // 16]
 
         def gather_wide(t, h):
             if h not in got:
-                got[h] = keep.tile([P, 2, WIDE], F32, name="got%d" % h, align_bytes=64)
-            nc.vector.tensor_copy(got[h][:, t, :], raw[t][:].indirect(offsets[:, h * WIDE // 16 : (h + 1) * WIDE // 16]))
+                got[h] = new([P, 2, WIDE], F32, "got%d" % h)
+            nc.vector.tensor_copy(got[h][:, t, :], raw[t][:].indirect(entries(h * WIDE, WIDE)))
 
-        def gather(t, q):
-            if q not in grouped:
-                tag = ("grouped0", "grouped1", "wgrouped1", "xscales1")[q]
-                grouped[q] = keep.tile([P, PACK * PIECE], BF16, name="grouped%d" % q, tag=tag, align_bytes=64)
-            dst = grouped[q][:].rearrange("p (j t) -> p j t", t=PACK)[:, :, t]
-            nc.scalar.activation(dst, bf23[:, t - 2, :].indirect(list_piece(q)), COPY)
+        def gather(t, i):
+            first, n = PIECES[i]
+            if i not in grouped:
+                grouped[i] = new([P, PACK * n], BF16, "grouped%d" % i)
+            dst = grouped[i][:].rearrange("p (j t) -> p j t", t=PACK)[:, :, t]
+            nc.scalar.activation(dst, bf23[:, t - 2, :].indirect(entries(first, n)), COPY)
 
-        def round_pair(copy, q, a, b):
-            first = (q % 2) * PIECE
-            dst = grouped[q][:].rearrange("p (j t) -> p j t", t=PACK)[:, a:b, 0:2]
-            copy(out=dst, in_=got[q // 2][:, :, first + a : first + b].rearrange("p t j -> p j t"))
+        def round_pair(i):
+            first, n = PIECES[i]
+            dst = grouped[i][:].rearrange("p (j t) -> p j t", t=PACK)[:, :, 0:2]
+            src = got[first // WIDE][:, :, first % WIDE : first % WIDE + n]
+            nc.scalar.copy(out=dst, in_=src.rearrange("p t j -> p j t"))
 
-        def interleave_weights(q):
-            wgrouped[q] = keep.tile(
-                [P, PACK * EXPERTS * N], BF16, name="wgrouped%d" % q, align_bytes=64
-            )
-            dst = wgrouped[q][:].rearrange("p (e c i t) -> p e c t i", e=EXPERTS, i=RUN, t=PACK)
-            first = (q % 2) * EXPERTS
-            src = wraw[q // 2][:, first : first + EXPERTS, :].rearrange("p e (t c i) -> p e c t i", t=PACK, i=RUN)
-            nc.vector.tensor_copy(out=dst, in_=src)
+        def interleave_weights(copy, q):
+            wgrouped[q] = new([P, PACK * PAIR * N], BF16, "wgrouped%d" % q)
+            dst = wgrouped[q][:].rearrange("p (e c i t) -> p e c t i", e=PAIR, i=RUN, t=PACK)
+            src = wraw0[:, q * PAIR : (q + 1) * PAIR, :] if q < LOAD_PAIRS else wraw1[:]
+            copy(out=dst, in_=src.rearrange("p e (t c i) -> p e c t i", t=PACK, i=RUN))
 
         def quantise_weights(q):
-            tag = ("wcodes0", "wcodes1", "grouped1", "wgrouped1")[q]
-            wcodes[q] = keep.tile([P, EXPERTS * N], U32, name="wcodes%d" % q, tag=tag, align_bytes=64)
+            wcodes[q] = new([P, PAIR * N], U32, "wcodes%d" % q)
             nc.vector.quantize_mx(out=wcodes[q][:].bitcast(FP8X4), scales=wscales[q][:], in_=wgrouped[q][:])
 
-        def quantise_tokens(q):
-            tag = ("wgrouped0", "wraw1", "late0", "late1")[q]
-            xcodes[q] = keep.tile([P, PIECE], U32, name="xcodes%d" % q, tag=tag, align_bytes=64)
-            nc.vector.quantize_mx(out=xcodes[q][:].bitcast(FP8X4), scales=xscales[q][:], in_=grouped[q][:])
+        def quantise_tokens(i):
+            xcodes[i] = new([P, PIECES[i][1]], U32, "xcodes%d" % i)
+            nc.vector.quantize_mx(out=xcodes[i][:].bitcast(FP8X4), scales=xscales[i][:], in_=grouped[i][:])
 
-        def multiply(q):
-            for e in range(EXPERTS):
+        def multiply(i):
+            first, n = PIECES[i]
+            for at in range(0, n, C):
+                q, e = divmod((first + at) // C, PAIR)
                 nc.tensor.matmul_mx(
-                    out=bank[q][:, e * C : (e + 1) * C],
+                    out=bank[i][:, at : at + C],
                     lhsT=wcodes[q][:, e * N : (e + 1) * N].bitcast(FP8X4),
                     lhsT_scale=wscales[q][:, e * N : (e + 1) * N],
-                    rhs=xcodes[q][:, e * C : (e + 1) * C].bitcast(FP8X4),
-                    rhs_scale=xscales[q][:, e * C : (e + 1) * C],
+                    rhs=xcodes[i][:, at : at + C].bitcast(FP8X4),
+                    rhs_scale=xscales[i][:, at : at + C],
                     start=True,
                     stop=True,
                 )
 
-        def empty_bank(q):
-            sums[q] = keep.tile([P, PIECE], F32, name="sums%d" % q, tag="late%d" % (q % 2), align_bytes=64)
-            if q < BANKS_ON_VECTOR:
-                nc.vector.tensor_copy(out=sums[q][:], in_=bank[q][:])
-            else:
-                nc.scalar.copy(out=sums[q][:], in_=bank[q][:])
+        def empty_bank(copy, i):
+            sums[i] = new([P, PIECES[i][1]], F32, "sums%d" % i)
+            copy(out=sums[i][:], in_=bank[i][:])
 
-        def scatter(q):
+        def scatter(i):
+            first, n = PIECES[i]
             nc.vector.tensor_tensor(
-                scattered[:].indirect(list_piece(q)), sums[q][:], gate_sb[:, q * PIECE : (q + 1) * PIECE], MULT
+                scattered[:].indirect(entries(first, n)), sums[i][:], gate_sb[:, first : first + n], MULT
             )
 
+        vector, scalar = nc.vector.tensor_copy, nc.scalar.copy
         spare = keep.tile([P, 2], F32, name="spare")
         nc.gpsimd.memset(spare[:, 0:1], 0.0)
-        nc.scalar.copy(out=spare[:, 1:2], in_=spare[:, 0:1])
+        scalar(out=spare[:, 1:2], in_=spare[:, 0:1])
         for c in range(PARTS):
-            nc.scalar.copy(out=bf23[:, 0, c * PART : (c + 1) * PART], in_=raw2[c][:])
+            scalar(out=bf23[:, 0, c * PART : (c + 1) * PART], in_=raw2[c][:])
         for t in (0, 1):
             for h in range(2):
                 gather_wide(t, h)
-        nc.vector.tensor_copy(out=bf23[:, 1, :], in_=raw[3][:])
+        vector(out=bf23[:, 1, :], in_=raw[3][:])
+        for i in range(2):
+            gather(2, i)
+        for i in range(2):
+            round_pair(i)
+        for i in range(2):
+            gather(3, i)
         for q in range(2):
-            gather(2, q)
+            interleave_weights(vector, q)
         for q in range(2):
-            round_pair(nc.scalar.copy, q, 0, PIECE)
-        for q in range(2):
-            gather(3, q)
-        for q in range(2):
-            interleave_weights(q)
             quantise_weights(q)
         quantise_tokens(0)
         multiply(0)
-        for q in range(2, PIECES):
-            interleave_weights(q)
+        interleave_weights(vector, 2)
         quantise_tokens(1)
         multiply(1)
-        empty_bank(0)
+        empty_bank(vector, 0)
         quantise_weights(2)
         gather(2, 2)
         gather(3, 2)
-        round_pair(nc.scalar.copy, 2, 0, PIECE)
+        round_pair(2)
         scatter(0)
         quantise_tokens(2)
         multiply(2)
-        empty_bank(1)
-        gather(2, LAST)
-        gather(3, LAST)
-        round_pair(nc.vector.tensor_copy, LAST, 0, LAST_ON_VECTOR)
-        round_pair(nc.scalar.copy, LAST, LAST_ON_VECTOR, PIECE)
+        empty_bank(scalar, 1)
+        interleave_weights(scalar, 3)
+        gather(2, 3)
+        gather(3, 3)
+        round_pair(3)
         scatter(1)
-        quantise_weights(LAST)
-        quantise_tokens(LAST)
-        multiply(LAST)
-        for q in range(2, PIECES):
-            empty_bank(q)
-            scatter(q)
+        quantise_weights(3)
+        quantise_tokens(3)
+        multiply(3)
+        empty_bank(scalar, 2)
+        gather(2, 4)
+        gather(3, 4)
+        round_pair(4)
+        scatter(2)
+        quantise_tokens(4)
+        multiply(4)
+        for i in (3, 4):
+            empty_bank(scalar, i)
+            scatter(i)
 
         nc.sync.dma_start(out, scattered[:])

@@ -24,7 +24,8 @@ RUN = 4
 WIDE = 2 * BANK
 PARTS = 2
 PART = T // PARTS
-LOAD_PAIRS = 3
+LOAD_PAIRS = 2
+PAIRED = 2
 
 
 def tile_routed_moe_kernel(tc, xT, w, gate, offs, out):
@@ -40,20 +41,20 @@ def tile_routed_moe_kernel(tc, xT, w, gate, offs, out):
         raw = {t: keep.tile([P, T], F32, name="raw%d" % t, align_bytes=64) for t in (0, 1, 3)}
         raw2 = [keep.tile([P, PART], F32, name="raw2_%d" % c, align_bytes=64) for c in range(PARTS)]
         w_rows = w.rearrange("e (p t) n -> p e (t n)", t=PACK)
-        wraw0 = keep.tile([P, LOAD_PAIRS * PAIR, PACK * N], F32, name="wraw0", align_bytes=64)
-        wraw1 = keep.tile([P, E - LOAD_PAIRS * PAIR, PACK * N], F32, name="wraw1", align_bytes=64)
+        wraw = [keep.tile([P, LOAD_PAIRS * PAIR, PACK * N], F32, name="wraw%d" % l, align_bytes=64) for l in range(PAIRS // LOAD_PAIRS)]
         gate_sb = keep.tile([P, E * C], F32, name="gate_sb")
         nc.sync.dma_start(raw[0][:], planes[:, 0, :])
         for c in range(PARTS):
             nc.sync.dma_start(raw2[c][:], planes[:, 2, c * PART : (c + 1) * PART])
         for t in (1, 3):
             nc.sync.dma_start(raw[t][:], planes[:, t, :])
-        nc.sync.dma_start(wraw0[:], w_rows[:, : LOAD_PAIRS * PAIR, :])
-        nc.sync.dma_start(wraw1[:], w_rows[:, LOAD_PAIRS * PAIR :, :])
+        for l in range(PAIRS // LOAD_PAIRS):
+            nc.sync.dma_start(wraw[l][:], w_rows[:, l * LOAD_PAIRS * PAIR : (l + 1) * LOAD_PAIRS * PAIR, :])
         nc.sync.dma_start(gate_sb[:], gate)
 
         bf23 = keep.tile([P, 2, T], BF16, name="bf23")
-        got = {}
+        pairs = keep.tile([P, 2, WIDE, 2], BF16, name="pairs", align_bytes=64)
+        late = keep.tile([P, 2, WIDE], F32, name="late", align_bytes=64)
         grouped = {}
         wgrouped = {}
         wcodes = {}
@@ -65,19 +66,16 @@ def tile_routed_moe_kernel(tc, xT, w, gate, offs, out):
         scattered = keep.tile([P, T], F32, name="scattered")
 
         TAGS = {
-            "grouped2": "wgrouped1",
+            "grouped2": "xscales0",
             "wgrouped3": "wscales1",
             "grouped3": "xscales1",
             "grouped4": "xscales2",
-            "sums3": "got1",
-            "xcodes0": "wgrouped0",
-            "xcodes1": "wraw0",
-            "wcodes2": "grouped1",
-            "sums0": "late0",
-            "xcodes2": "late0",
-            "sums2": "late0",
-            "sums1": "late1",
-            "xcodes3": "late1",
+            "sums3": "late",
+            "grouped0": "wraw0",
+            "sums0": "sums0",
+            "xcodes2": "sums0",
+            "sums2": "sums0",
+            "xcodes3": "sums1",
         }
 
         def new(shape, dtype, name):
@@ -87,27 +85,35 @@ def tile_routed_moe_kernel(tc, xT, w, gate, offs, out):
             return offsets[:, first // 16 : (first + n) // 16]
 
         def gather_wide(t, h):
-            if h not in got:
-                got[h] = new([P, 2, WIDE], F32, "got%d" % h)
-            nc.vector.tensor_copy(got[h][:, t, :], raw[t][:].indirect(entries(h * WIDE, WIDE)))
+            dst = pairs[:, 0, :, t] if h == 0 else late[:, t, :]
+            nc.vector.tensor_copy(dst, raw[t][:].indirect(entries(h * WIDE, WIDE)))
 
         def gather(t, i):
             first, n = PIECES[i]
-            if i not in grouped:
-                grouped[i] = new([P, PACK * n], BF16, "grouped%d" % i)
-            dst = grouped[i][:].rearrange("p (j t) -> p j t", t=PACK)[:, :, t]
+            if i < PAIRED:
+                dst = pairs[:, 1, first : first + n, t - 2]
+            else:
+                if i not in grouped:
+                    grouped[i] = new([P, PACK * n], BF16, "grouped%d" % i)
+                dst = grouped[i][:].rearrange("p (j t) -> p j t", t=PACK)[:, :, t]
             nc.scalar.activation(dst, bf23[:, t - 2, :].indirect(entries(first, n)), COPY)
 
-        def round_pair(i):
+        def merge(i):
             first, n = PIECES[i]
-            dst = grouped[i][:].rearrange("p (j t) -> p j t", t=PACK)[:, :, 0:2]
-            src = got[first // WIDE][:, :, first % WIDE : first % WIDE + n]
-            nc.scalar.copy(out=dst, in_=src.rearrange("p t j -> p j t"))
+            grouped[i] = new([P, PACK * n], BF16, "grouped%d" % i)
+            dst = grouped[i][:].rearrange("p (j u t) -> p j u t", u=2, t=2)
+            nc.vector.tensor_copy(out=dst, in_=pairs[:, :, first : first + n, :].rearrange("p u j t -> p j u t"))
+
+        def round_pair(copy, i, a, b):
+            first = PIECES[i][0] - WIDE
+            dst = grouped[i][:].rearrange("p (j t) -> p j t", t=PACK)[:, a:b, 0:2]
+            copy(out=dst, in_=late[:, :, first + a : first + b].rearrange("p t j -> p j t"))
 
         def interleave_weights(copy, q):
             wgrouped[q] = new([P, PACK * PAIR * N], BF16, "wgrouped%d" % q)
             dst = wgrouped[q][:].rearrange("p (e c i t) -> p e c t i", e=PAIR, i=RUN, t=PACK)
-            src = wraw0[:, q * PAIR : (q + 1) * PAIR, :] if q < LOAD_PAIRS else wraw1[:]
+            at = q % LOAD_PAIRS * PAIR
+            src = wraw[q // LOAD_PAIRS][:, at : at + PAIR, :]
             copy(out=dst, in_=src.rearrange("p e (t c i) -> p e c t i", t=PACK, i=RUN))
 
         def quantise_weights(q):
@@ -151,35 +157,36 @@ def tile_routed_moe_kernel(tc, xT, w, gate, offs, out):
         for t in (0, 1):
             for h in range(2):
                 gather_wide(t, h)
-        vector(out=bf23[:, 1, :], in_=raw[3][:])
-        for i in range(2):
+        for i in range(PAIRED):
             gather(2, i)
-        for i in range(2):
-            round_pair(i)
-        for i in range(2):
+        scalar(out=bf23[:, 1, :], in_=raw[3][:])
+        for i in range(PAIRED):
             gather(3, i)
-        for q in range(2):
-            interleave_weights(vector, q)
-        for q in range(2):
-            quantise_weights(q)
+        interleave_weights(vector, 0)
+        interleave_weights(vector, 1)
+        quantise_weights(0)
+        merge(0)
+        quantise_weights(1)
         quantise_tokens(0)
         multiply(0)
-        interleave_weights(vector, 2)
+        merge(1)
         quantise_tokens(1)
         multiply(1)
-        empty_bank(vector, 0)
-        quantise_weights(2)
+        empty_bank(scalar, 0)
         gather(2, 2)
         gather(3, 2)
-        round_pair(2)
+        round_pair(vector, 2, 0, BANK // 2)
+        round_pair(scalar, 2, BANK // 2, BANK)
+        interleave_weights(scalar, 2)
         scatter(0)
+        quantise_weights(2)
         quantise_tokens(2)
         multiply(2)
         empty_bank(scalar, 1)
         interleave_weights(scalar, 3)
         gather(2, 3)
         gather(3, 3)
-        round_pair(3)
+        round_pair(scalar, 3, 0, C)
         scatter(1)
         quantise_weights(3)
         quantise_tokens(3)
@@ -187,7 +194,7 @@ def tile_routed_moe_kernel(tc, xT, w, gate, offs, out):
         empty_bank(scalar, 2)
         gather(2, 4)
         gather(3, 4)
-        round_pair(4)
+        round_pair(scalar, 4, 0, C)
         scatter(2)
         quantise_tokens(4)
         multiply(4)

@@ -21,11 +21,12 @@ PAIR = BANK // C
 PAIRS = E // PAIR
 PIECES = ((0, BANK), (BANK, BANK), (2 * BANK, BANK), (3 * BANK, C), (3 * BANK + C, C))
 RUN = 4
-WIDE = 2 * BANK
 PARTS = 2
 PART = T // PARTS
 LOAD_PAIRS = 2
-PAIRED = 2
+PAIRED = 3
+HEAD = sum(n for first, n in PIECES[:PAIRED])
+MERGES_ON_VECTOR = 2
 
 
 def tile_routed_moe_kernel(tc, xT, w, gate, offs, out):
@@ -35,7 +36,6 @@ def tile_routed_moe_kernel(tc, xT, w, gate, offs, out):
         psum = ctx.enter_context(tc.psum_pool(name="psum", bufs=1))
 
         offsets = keep.tile([P, E * C // 16], U16, name="offsets")
-        nc.sync.dma_start(offsets[:], offs)
 
         planes = xT.rearrange("(p t) n -> p t n", t=PACK)
         raw = {t: keep.tile([P, T], F32, name="raw%d" % t, align_bytes=64) for t in (0, 1, 3)}
@@ -44,6 +44,7 @@ def tile_routed_moe_kernel(tc, xT, w, gate, offs, out):
         wraw = [keep.tile([P, LOAD_PAIRS * PAIR, PACK * N], F32, name="wraw%d" % l, align_bytes=64) for l in range(PAIRS // LOAD_PAIRS)]
         gate_sb = keep.tile([P, E * C], F32, name="gate_sb")
         nc.sync.dma_start(raw[0][:], planes[:, 0, :])
+        nc.sync.dma_start(offsets[:], offs)
         for c in range(PARTS):
             nc.sync.dma_start(raw2[c][:], planes[:, 2, c * PART : (c + 1) * PART])
         for t in (1, 3):
@@ -53,8 +54,8 @@ def tile_routed_moe_kernel(tc, xT, w, gate, offs, out):
         nc.sync.dma_start(gate_sb[:], gate)
 
         bf23 = keep.tile([P, 2, T], BF16, name="bf23")
-        pairs = keep.tile([P, 2, WIDE, 2], BF16, name="pairs", align_bytes=64)
-        late = keep.tile([P, 2, WIDE], F32, name="late", align_bytes=64)
+        pairs = keep.tile([P, 2, HEAD, 2], BF16, name="pairs", align_bytes=64)
+        late = keep.tile([P, 2, E * C - HEAD], F32, name="late", align_bytes=64)
         grouped = {}
         wgrouped = {}
         wcodes = {}
@@ -72,9 +73,8 @@ def tile_routed_moe_kernel(tc, xT, w, gate, offs, out):
             "grouped4": "xscales2",
             "sums3": "late",
             "grouped0": "wraw0",
-            "sums0": "sums0",
-            "xcodes2": "sums0",
-            "sums2": "sums0",
+            "grouped1": "wraw0",
+            "wgrouped2": "wraw0",
             "xcodes3": "sums1",
         }
 
@@ -84,9 +84,9 @@ def tile_routed_moe_kernel(tc, xT, w, gate, offs, out):
         def entries(first, n):
             return offsets[:, first // 16 : (first + n) // 16]
 
-        def gather_wide(t, h):
-            dst = pairs[:, 0, :, t] if h == 0 else late[:, t, :]
-            nc.vector.tensor_copy(dst, raw[t][:].indirect(entries(h * WIDE, WIDE)))
+        def gather_wide(t):
+            nc.vector.tensor_copy(pairs[:, 0, :, t], raw[t][:].indirect(entries(0, HEAD)))
+            nc.vector.tensor_copy(late[:, t, :], raw[t][:].indirect(entries(HEAD, E * C - HEAD)))
 
         def gather(t, i):
             first, n = PIECES[i]
@@ -101,13 +101,14 @@ def tile_routed_moe_kernel(tc, xT, w, gate, offs, out):
         def merge(i):
             first, n = PIECES[i]
             grouped[i] = new([P, PACK * n], BF16, "grouped%d" % i)
+            copy = nc.vector.tensor_copy if i < MERGES_ON_VECTOR else nc.scalar.copy
             dst = grouped[i][:].rearrange("p (j u t) -> p j u t", u=2, t=2)
-            nc.vector.tensor_copy(out=dst, in_=pairs[:, :, first : first + n, :].rearrange("p u j t -> p j u t"))
+            copy(out=dst, in_=pairs[:, :, first : first + n, :].rearrange("p u j t -> p j u t"))
 
-        def round_pair(copy, i, a, b):
-            first = PIECES[i][0] - WIDE
-            dst = grouped[i][:].rearrange("p (j t) -> p j t", t=PACK)[:, a:b, 0:2]
-            copy(out=dst, in_=late[:, :, first + a : first + b].rearrange("p t j -> p j t"))
+        def round_pair(i):
+            first, n = PIECES[i][0] - HEAD, PIECES[i][1]
+            dst = grouped[i][:].rearrange("p (j t) -> p j t", t=PACK)[:, :, 0:2]
+            nc.scalar.copy(out=dst, in_=late[:, :, first : first + n].rearrange("p t j -> p j t"))
 
         def interleave_weights(copy, q):
             wgrouped[q] = new([P, PACK * PAIR * N], BF16, "wgrouped%d" % q)
@@ -155,13 +156,12 @@ def tile_routed_moe_kernel(tc, xT, w, gate, offs, out):
         for c in range(PARTS):
             scalar(out=bf23[:, 0, c * PART : (c + 1) * PART], in_=raw2[c][:])
         for t in (0, 1):
-            for h in range(2):
-                gather_wide(t, h)
+            gather_wide(t)
         for i in range(PAIRED):
             gather(2, i)
         scalar(out=bf23[:, 1, :], in_=raw[3][:])
-        for i in range(PAIRED):
-            gather(3, i)
+        gather(3, 0)
+        gather(3, 1)
         interleave_weights(vector, 0)
         interleave_weights(vector, 1)
         quantise_weights(0)
@@ -173,20 +173,18 @@ def tile_routed_moe_kernel(tc, xT, w, gate, offs, out):
         quantise_tokens(1)
         multiply(1)
         empty_bank(scalar, 0)
-        gather(2, 2)
         gather(3, 2)
-        round_pair(vector, 2, 0, BANK // 2)
-        round_pair(scalar, 2, BANK // 2, BANK)
+        merge(2)
         interleave_weights(scalar, 2)
         scatter(0)
-        quantise_weights(2)
         quantise_tokens(2)
+        quantise_weights(2)
         multiply(2)
         empty_bank(scalar, 1)
         interleave_weights(scalar, 3)
         gather(2, 3)
         gather(3, 3)
-        round_pair(scalar, 3, 0, C)
+        round_pair(3)
         scatter(1)
         quantise_weights(3)
         quantise_tokens(3)
@@ -194,7 +192,7 @@ def tile_routed_moe_kernel(tc, xT, w, gate, offs, out):
         empty_bank(scalar, 2)
         gather(2, 4)
         gather(3, 4)
-        round_pair(scalar, 4, 0, C)
+        round_pair(4)
         scatter(2)
         quantise_tokens(4)
         multiply(4)

@@ -73,8 +73,6 @@ def tile_routed_moe_kernel(tc, xT, w, gate, offs, out):
             "grouped4": "xscales2",
             "sums3": "late",
             "grouped0": "wraw0",
-            "grouped1": "wraw0",
-            "wgrouped2": "wraw0",
             "xcodes3": "sums1",
         }
 
@@ -170,15 +168,15 @@ def tile_routed_moe_kernel(tc, xT, w, gate, offs, out):
         quantise_tokens(0)
         multiply(0)
         merge(1)
+        interleave_weights(vector, 2)
         quantise_tokens(1)
         multiply(1)
         empty_bank(scalar, 0)
         gather(3, 2)
         merge(2)
-        interleave_weights(scalar, 2)
+        quantise_weights(2)
         scatter(0)
         quantise_tokens(2)
-        quantise_weights(2)
         multiply(2)
         empty_bank(scalar, 1)
         interleave_weights(scalar, 3)

from contextlib import ExitStack

import concourse.mybir as mybir

K, T, E, C, N = 512, 2048, 8, 256, 128
FLOPS = 2 * K * N * E * C

F32 = mybir.dt.float32
BF16 = mybir.dt.bfloat16
U32 = mybir.dt.uint32
U16 = mybir.dt.uint16
U8 = mybir.dt.uint8
FP8X4 = mybir.dt.float8_e4m3fn_x4
MULT = mybir.AluOpType.mult
COPY = mybir.ActivationFunctionType.Copy

P = 128
PACK = 4
BANK = 512
PAIR = BANK // C
PAIRS = E // PAIR
PIECES = ((0, BANK), (BANK, BANK), (2 * BANK, BANK), (3 * BANK, C), (3 * BANK + C, C))
RUN = 4
PARTS = 2
PART = T // PARTS
LOAD_PAIRS = 2
PAIRED = 3
HEAD = sum(n for first, n in PIECES[:PAIRED])
MERGES_ON_VECTOR = 2


def tile_routed_moe_kernel(tc, xT, w, gate, offs, out):
    nc = tc.nc
    with ExitStack() as ctx:
        keep = ctx.enter_context(tc.tile_pool(name="keep", bufs=1))
        psum = ctx.enter_context(tc.psum_pool(name="psum", bufs=1))

        offsets = keep.tile([P, E * C // 16], U16, name="offsets")

        planes = xT.rearrange("(p t) n -> p t n", t=PACK)
        raw = {t: keep.tile([P, T], F32, name="raw%d" % t, align_bytes=64) for t in (0, 1, 3)}
        raw2 = [keep.tile([P, PART], F32, name="raw2_%d" % c, align_bytes=64) for c in range(PARTS)]
        w_rows = w.rearrange("e (p t) n -> p e (t n)", t=PACK)
        wraw = [keep.tile([P, LOAD_PAIRS * PAIR, PACK * N], F32, name="wraw%d" % l, align_bytes=64) for l in range(PAIRS // LOAD_PAIRS)]
        gate_sb = keep.tile([P, E * C], F32, name="gate_sb")
        nc.sync.dma_start(raw[0][:], planes[:, 0, :])
        nc.sync.dma_start(offsets[:], offs)
        for c in range(PARTS):
            nc.sync.dma_start(raw2[c][:], planes[:, 2, c * PART : (c + 1) * PART])
        for t in (1, 3):
            nc.sync.dma_start(raw[t][:], planes[:, t, :])
        for l in range(PAIRS // LOAD_PAIRS):
            nc.sync.dma_start(wraw[l][:], w_rows[:, l * LOAD_PAIRS * PAIR : (l + 1) * LOAD_PAIRS * PAIR, :])
        nc.sync.dma_start(gate_sb[:], gate)

        bf23 = keep.tile([P, 2, T], BF16, name="bf23")
        pairs = keep.tile([P, 2, HEAD, 2], BF16, name="pairs", align_bytes=64)
        late = keep.tile([P, 2, E * C - HEAD], F32, name="late", align_bytes=64)
        grouped = {}
        wgrouped = {}
        wcodes = {}
        wscales = [keep.tile([P, PAIR * N], U8, name="wscales%d" % q, align_bytes=64) for q in range(PAIRS)]
        xcodes = {}
        xscales = [keep.tile([P, PIECES[i][1]], U8, name="xscales%d" % i, align_bytes=64) for i in range(len(PIECES))]
        bank = [psum.tile([P, PIECES[i][1]], F32, name="bank%d" % i) for i in range(len(PIECES))]
        sums = {}
        scattered = keep.tile([P, T], F32, name="scattered")

        TAGS = {
            "grouped2": "xscales0",
            "wgrouped3": "wscales1",
            "grouped3": "xscales1",
            "grouped4": "xscales2",
            "sums3": "late",
            "grouped0": "wraw0",
            "xcodes3": "sums1",
        }

        def new(shape, dtype, name):
            return keep.tile(shape, dtype, name=name, tag=TAGS.get(name, name), align_bytes=64)

        def entries(first, n):
            return offsets[:, first // 16 : (first + n) // 16]

        def gather_wide(t):
            nc.vector.tensor_copy(pairs[:, 0, :, t], raw[t][:].indirect(entries(0, HEAD)))
            nc.vector.tensor_copy(late[:, t, :], raw[t][:].indirect(entries(HEAD, E * C - HEAD)))

        def gather(t, i):
            first, n = PIECES[i]
            if i < PAIRED:
                dst = pairs[:, 1, first : first + n, t - 2]
            else:
                if i not in grouped:
                    grouped[i] = new([P, PACK * n], BF16, "grouped%d" % i)
                dst = grouped[i][:].rearrange("p (j t) -> p j t", t=PACK)[:, :, t]
            nc.scalar.activation(dst, bf23[:, t - 2, :].indirect(entries(first, n)), COPY)

        def merge(i):
            first, n = PIECES[i]
            grouped[i] = new([P, PACK * n], BF16, "grouped%d" % i)
            copy = nc.vector.tensor_copy if i < MERGES_ON_VECTOR else nc.scalar.copy
            dst = grouped[i][:].rearrange("p (j u t) -> p j u t", u=2, t=2)
            copy(out=dst, in_=pairs[:, :, first : first + n, :].rearrange("p u j t -> p j u t"))

        def round_pair(i):
            first, n = PIECES[i][0] - HEAD, PIECES[i][1]
            dst = grouped[i][:].rearrange("p (j t) -> p j t", t=PACK)[:, :, 0:2]
            nc.scalar.copy(out=dst, in_=late[:, :, first : first + n].rearrange("p t j -> p j t"))

        def interleave_weights(copy, q):
            wgrouped[q] = new([P, PACK * PAIR * N], BF16, "wgrouped%d" % q)
            dst = wgrouped[q][:].rearrange("p (e c i t) -> p e c t i", e=PAIR, i=RUN, t=PACK)
            at = q % LOAD_PAIRS * PAIR
            src = wraw[q // LOAD_PAIRS][:, at : at + PAIR, :]
            copy(out=dst, in_=src.rearrange("p e (t c i) -> p e c t i", t=PACK, i=RUN))

        def quantise_weights(q):
            wcodes[q] = new([P, PAIR * N], U32, "wcodes%d" % q)
            nc.vector.quantize_mx(out=wcodes[q][:].bitcast(FP8X4), scales=wscales[q][:], in_=wgrouped[q][:])

        def quantise_tokens(i):
            xcodes[i] = new([P, PIECES[i][1]], U32, "xcodes%d" % i)
            nc.vector.quantize_mx(out=xcodes[i][:].bitcast(FP8X4), scales=xscales[i][:], in_=grouped[i][:])

        def multiply(i):
            first, n = PIECES[i]
            for at in range(0, n, C):
                q, e = divmod((first + at) // C, PAIR)
                nc.tensor.matmul_mx(
                    out=bank[i][:, at : at + C],
                    lhsT=wcodes[q][:, e * N : (e + 1) * N].bitcast(FP8X4),
                    lhsT_scale=wscales[q][:, e * N : (e + 1) * N],
                    rhs=xcodes[i][:, at : at + C].bitcast(FP8X4),
                    rhs_scale=xscales[i][:, at : at + C],
                    start=True,
                    stop=True,
                )

        def empty_bank(copy, i):
            sums[i] = new([P, PIECES[i][1]], F32, "sums%d" % i)
            copy(out=sums[i][:], in_=bank[i][:])

        def scatter(i):
            first, n = PIECES[i]
            nc.vector.tensor_tensor(
                scattered[:].indirect(entries(first, n)), sums[i][:], gate_sb[:, first : first + n], MULT
            )

        vector, scalar = nc.vector.tensor_copy, nc.scalar.copy
        spare = keep.tile([P, 2], F32, name="spare")
        nc.gpsimd.memset(spare[:, 0:1], 0.0)
        scalar(out=spare[:, 1:2], in_=spare[:, 0:1])
        for c in range(PARTS):
            scalar(out=bf23[:, 0, c * PART : (c + 1) * PART], in_=raw2[c][:])
        for t in (0, 1):
            gather_wide(t)
        for i in range(PAIRED):
            gather(2, i)
        scalar(out=bf23[:, 1, :], in_=raw[3][:])
        gather(3, 0)
        gather(3, 1)
        interleave_weights(vector, 0)
        interleave_weights(vector, 1)
        quantise_weights(0)
        merge(0)
        quantise_weights(1)
        quantise_tokens(0)
        multiply(0)
        merge(1)
        interleave_weights(vector, 2)
        quantise_tokens(1)
        multiply(1)
        empty_bank(scalar, 0)
        gather(3, 2)
        merge(2)
        quantise_weights(2)
        scatter(0)
        quantise_tokens(2)
        multiply(2)
        empty_bank(scalar, 1)
        interleave_weights(scalar, 3)
        gather(2, 3)
        gather(3, 3)
        round_pair(3)
        scatter(1)
        quantise_weights(3)
        quantise_tokens(3)
        multiply(3)
        empty_bank(scalar, 2)
        gather(2, 4)
        gather(3, 4)
        round_pair(4)
        scatter(2)
        quantise_tokens(4)
        multiply(4)
        for i in (3, 4):
            empty_bank(scalar, i)
            scatter(i)

        nc.sync.dma_start(out, scattered[:])
